import numpy as np
import ml_dtypes


def mxq(x, axis, fmt="e4m3"):
    dtype, down = {"e4m3": (ml_dtypes.float8_e4m3fn, 7), "e5m2": (ml_dtypes.float8_e5m2, 14)}[fmt]
    v = np.moveaxis(np.asarray(x, np.float32).astype(ml_dtypes.bfloat16).astype(np.float64), axis, -1)
    blocks = v.reshape(v.shape[:-1] + (-1, 32))
    amax = np.abs(blocks).max(-1, keepdims=True)
    byte = np.maximum(np.where(amax > 0, np.frexp(amax)[1] - 1 + 127, 0) - down, 1)
    scale = np.exp2(byte - 127.0)
    codes = (blocks / scale).astype(np.float32).astype(dtype).astype(np.float64)
    return np.moveaxis((codes * scale).reshape(v.shape), -1, axis)


WIDE = False


def mx_kscale(k):
    if not WIDE:
        return np.ones(k)
    levels = np.array([24, -24, 12, -12, 0])
    if k % 512:
        return np.exp2(np.random.permutation(np.resize(levels, k // 32))).repeat(32)
    a = np.empty((k // 512, 16))
    for p in range(k // 512):
        a[p, :8] = np.random.permutation(np.resize(levels, 8))
        for g in range(8):
            far = levels[np.abs(levels - a[p, g]) >= 10]
            a[p, g + 8] = far[np.random.randint(len(far))]
    return np.exp2(a.ravel()).repeat(32)


def f64(x):
    return np.asarray(x).astype(np.float64)


def striped(idx):
    return np.tile(idx.reshape(-1, 16).T, (8, 1)).astype(np.uint16)


def unstriped(offs):
    return offs[:16].T.reshape(-1).astype(np.int64)


E2M1 = np.array([0.0, 0.5, 1.0, 1.5, 2.0, 3.0, 4.0, 6.0, -0.0, -0.5, -1.0, -1.5, -2.0, -3.0, -4.0, -6.0])


def pack_weight(w, fmt):
    k, n = w.shape
    w = f64(np.asarray(w, np.float32).astype(ml_dtypes.bfloat16)).reshape(k // 32, 32, n)
    amax = np.abs(w).max(1)
    if fmt == "e4m3":
        byte = np.frexp(amax)[1] - 1 + 127 - 7
    else:
        mant, ex = np.frexp(amax / 6.0)
        byte = np.where(mant > 0.5, ex, ex - 1) + 127
    byte = np.clip(np.where(amax > 0, byte, 1), 1, 254)
    scaled = (w * np.exp2(127.0 - byte)[:, None, :]).reshape(k, n).astype(np.float32)
    by_word = np.ascontiguousarray(scaled.reshape(k // 512, 128, 4, n).transpose(0, 1, 3, 2))
    if fmt == "e4m3":
        words = by_word.astype(ml_dtypes.float8_e4m3fn).view(np.uint8)
    else:
        c = by_word.astype(ml_dtypes.float4_e2m1fn).view(np.uint8) & 0xF
        words = (c[..., 0::2] | (c[..., 1::2] << 4)).reshape(k // 512, 128, 2 * n)
    return np.ascontiguousarray(words), np.ascontiguousarray(byte.astype(np.uint8).reshape(k // 512, 16, n))


def unpack_weight(words, scales, fmt):
    g, _, n = scales.shape
    words = np.ascontiguousarray(words).reshape(g, 128, n, -1)
    if fmt == "e4m3":
        vals = words.view(ml_dtypes.float8_e4m3fn).astype(np.float64)
    else:
        nib = np.empty((g, 128, n, 4), np.uint8)
        nib[..., 0::2] = words & 0xF
        nib[..., 1::2] = words >> 4
        vals = E2M1[nib]
    vals = vals * np.repeat(np.exp2(scales.astype(np.float64) - 127.0), 8, axis=1)[..., None]
    return vals.transpose(0, 1, 3, 2).reshape(g * 512, n)


def planes(y):
    n, m = y.shape
    v = y.astype(np.float32).astype(ml_dtypes.bfloat16).astype(np.float64).reshape(n // 32, 32, m)
    top = np.abs(v).max(1)
    byte = np.clip(np.where(top > 0, np.frexp(top)[1] - 1 + 127 - 7, 1), 1, 254)
    codes = (v * np.exp2(127.0 - byte)[:, None, :]).reshape(n, m).astype(np.float32).astype(ml_dtypes.float8_e4m3fn).view(np.uint8)
    words = codes.reshape(n // 512, 128, 4, m).transpose(0, 1, 3, 2)
    return np.ascontiguousarray(words), np.ascontiguousarray(byte.astype(np.uint8).reshape(n // 512, 16, m))


def sigm(f):
    return 1.0 / (1.0 + np.exp(-np.maximum(f, -700.0)))


K, N, T, J = 512, 512, 2048, 1024


def setup_inputs():
    n = np.random.standard_normal
    s = mx_kscale(K)[:, None]
    p_tab = pack_weight(n((K, T)) * s, "e4m3")
    p_wb = pack_weight(n((K, N)) / np.sqrt(2 * K) / s, "e4m3")
    p_wc = pack_weight(n((K, N)) / np.sqrt(K) / s, "e4m3")
    return {
        "tab_words": p_tab[0],
        "tab_scales": p_tab[1],
        "wa": (n((K, N)) / np.sqrt(2 * K) / s).astype(np.float32),
        "wb_words": p_wb[0],
        "wb_scales": p_wb[1],
        "wc_words": p_wc[0],
        "wc_scales": p_wc[1],
        "wgo": np.tile(np.random.uniform(0.5, 2.0, J), (128, 1)).astype(np.float32),
        "offs": striped(np.random.permutation(T)[:J]),
        "offs2": striped(np.random.permutation(T)[:J]),
    }


def reference(tab_words, tab_scales, wa, wb_words, wb_scales, wc_words, wc_scales, wgo, offs, offs2):
    idx = unstriped(offs)
    idx2 = unstriped(offs2)
    tab_ = unpack_weight(tab_words, tab_scales, "e4m3")[:, idx]
    tabb_ = unpack_weight(tab_words, tab_scales, "e4m3")[:, idx2]
    wa_ = mxq(f64(wa), 0, "e4m3")
    wb_ = unpack_weight(wb_words, wb_scales, "e4m3")
    za = wa_.T @ tabb_ + wb_.T @ tab_
    eta = sigm(za)
    wc_ = unpack_weight(wc_words, wc_scales, "e4m3")
    ms = wc_.T @ tab_
    out = np.zeros((N, T))
    out[:, idx2] = f64(wgo)[0] * (eta * ms)
    return (out,) + planes(out)

@@ -1,0 +1,242 @@
+from contextlib import ExitStack
+
+import concourse.mybir as mybir
+from concourse.masks import make_identity
+
+K, N, T, J = 512, 512, 2048, 1024
+FLOPS = 3 * 2 * K * N * J
+
+F32 = mybir.dt.float32
+BF16 = mybir.dt.bfloat16
+I32 = mybir.dt.int32
+U32 = mybir.dt.uint32
+U16 = mybir.dt.uint16
+U8 = mybir.dt.uint8
+FP8X4 = mybir.dt.float8_e4m3fn_x4
+ACT = mybir.ActivationFunctionType
+MULT = mybir.AluOpType.mult
+
+P = 128
+PACK = 4
+HALF = J // 2
+LIST_COLS = J // 16
+CHUNK = 512
+CHUNKS = T // CHUNK
+
+
+def load_scale_rows(queue, plane, rows):
+    for q in range(4):
+        queue.dma_start(out=plane[32 * q : 32 * q + 4, :].bitcast(I32), in_=rows[4 * q : 4 * q + 4, :].bitcast(I32))
+
+
+def words_of(packed):
+    return packed[0].rearrange("p c i -> p (c i)").bitcast(I32)
+
+
+def tile_list_rgg_noneP_kernel(
+    tc, tab_words, tab_scales, wa, wb_words, wb_scales, wc_words, wc_scales, wgo, offs, offs2, out_0, out_1, out_2
+):
+    nc = tc.nc
+    with ExitStack() as ctx:
+        keep = ctx.enter_context(tc.tile_pool(name="keep", bufs=1))
+        psum = ctx.enter_context(tc.psum_pool(name="psum", bufs=1))
+
+        src_list = keep.tile([P, LIST_COLS], U16, name="src_list")
+        dst_list = keep.tile([P, LIST_COLS], U16, name="dst_list")
+        tab_s = keep.tile([P, T], U8, name="tab_s", tag="page2_bytes", align_bytes=64)
+        tab_w = keep.tile([P, T], I32, name="tab_w", tag="page1_bytes", align_bytes=64)
+        wa_raw = keep.tile([P, PACK, N], F32, name="wa_raw")
+        w_scales = keep.tile([P, 2 * N], U8, name="w_scales", align_bytes=64)
+        ident = keep.tile([P, P], F32, name="ident")
+        wgo_rows = keep.tile([P, P], F32, name="wgo_rows")
+
+        nc.vector.memset(tab_s[:].bitcast(I32), 0)
+        nc.sync.dma_start(out=src_list[:], in_=offs)
+        load_scale_rows(nc.sync, tab_s, tab_scales[0])
+        nc.sync.dma_start(out=dst_list[:], in_=offs2)
+        nc.sync.dma_start(out=wa_raw[:], in_=wa.rearrange("(p j) n -> p j n", j=PACK))
+        nc.sync.dma_start(out=tab_w[:], in_=words_of(tab_words))
+
+        nc.gpsimd.memset(wgo_rows[:], 0.0)
+        make_identity(nc, ident[:])
+        warm = keep.tile([P, 1], F32, name="warm", tag="w_words", align_bytes=64)
+        nc.scalar.activation(out=warm[:], in_=ident[:, 0:1], func=ACT.Sigmoid)
+
+        page = [keep.tile([P, T], F32, name="page%d" % t, align_bytes=64) for t in range(1)]
+        nc.vector.memset(page[0][:], 0.0)
+        nc.vector.memset(w_scales[:].bitcast(I32), 0)
+
+        w_words = keep.tile([P, 2 * N], I32, name="w_words", tag="w_words", align_bytes=64)
+        wc_w, wb_w = w_words[:, 0:N], w_words[:, N : 2 * N]
+        nc.sync.dma_start(out=wc_w, in_=words_of(wc_words))
+        load_scale_rows(nc.sync, w_scales[:, 0:N], wc_scales[0])
+        nc.sync.dma_start(out=wgo_rows[0 : J // P, :], in_=wgo[0:1, :].rearrange("o (c p) -> (o c) p", p=P))
+        nc.sync.dma_start(out=wb_w, in_=words_of(wb_words))
+        load_scale_rows(nc.sync, w_scales[:, N : 2 * N], wb_scales[0])
+        wc_s = w_scales[:, 0:N]
+
+        wa_bf = keep.tile([P, N * PACK], BF16, name="wa_bf", align_bytes=64)
+        nc.scalar.copy(
+            out=wa_bf[:].rearrange("p (t m j) -> p m t j", t=PACK, j=PACK),
+            in_=wa_raw[:].rearrange("p j (m t) -> p m t j", t=PACK),
+        )
+
+        wgo_bank = psum.tile([P, HALF], F32, name="wgo_bank", tag="back0")
+        nc.tensor.transpose(wgo_bank[:, 0:P], wgo_rows[:], ident[:])
+        wgo_col = keep.tile([P, J // P], F32, name="wgo_col")
+        nc.scalar.copy(out=wgo_col[:], in_=wgo_bank[:, 0 : J // P])
+
+        src_s = keep.tile([P, J], U8, name="src_s", align_bytes=64)
+        src_w = [keep.tile([P, HALF], U32, name="src_w%d" % h, align_bytes=64) for h in range(2)]
+        dst_s = [keep.tile([P, HALF], U8, name="dst_s%d" % h, align_bytes=64) for h in range(2)]
+        dst_w = [keep.tile([P, HALF], U32, name="dst_w%d" % h, align_bytes=64) for h in range(2)]
+        half_cols = [slice(h * LIST_COLS // 2, (h + 1) * LIST_COLS // 2) for h in range(2)]
+        tab_u = tab_w[:].bitcast(U32)
+
+        nc.vector.tensor_copy(src_s[:], tab_s[:].indirect(src_list[:]))
+        nc.vector.tensor_copy(dst_s[0][:], tab_s[:].indirect(dst_list[:, half_cols[0]]))
+        nc.vector.tensor_copy(src_w[0][:], tab_u.indirect(src_list[:, half_cols[0]]))
+        nc.vector.tensor_copy(dst_w[0][:], tab_u.indirect(dst_list[:, half_cols[0]]))
+
+        wa_w = keep.tile([P, N], U32, name="wa_w", align_bytes=64)
+        wa_s = keep.tile([P, N], U8, name="wa_s", align_bytes=64)
+        nc.vector.quantize_mx(out=wa_w[:].bitcast(FP8X4), scales=wa_s[:], in_=wa_bf[:])
+        wbd_w = keep.tile([P, N], I32, name="wbd_w", align_bytes=64)
+        wbd_s = keep.tile([P, N], U8, name="wbd_s", align_bytes=64)
+        nc.vector.tensor_copy(out=wbd_w[:].rearrange("p (t m) -> p t m", t=PACK), in_=wb_w.rearrange("p (m t) -> p t m", t=PACK))
+        nc.vector.tensor_copy(
+            out=wbd_s[:].rearrange("p (t m) -> p t m", t=PACK),
+            in_=w_scales[:, N : 2 * N].rearrange("p (m t) -> p t m", t=PACK),
+        )
+
+        nc.vector.tensor_copy(src_w[1][:], tab_u.indirect(src_list[:, half_cols[1]]))
+        nc.vector.tensor_copy(dst_w[1][:], tab_u.indirect(dst_list[:, half_cols[1]]))
+        nc.vector.tensor_copy(dst_s[1][:], tab_s[:].indirect(dst_list[:, half_cols[1]]))
+
+        page.append(keep.tile([P, T], F32, name="page1", tag="page1_bytes", align_bytes=64))
+        page.append(keep.tile([P, T], F32, name="page2", tag="page2_bytes", align_bytes=64))
+        nc.gpsimd.memset(page[1][:], 0.0)
+        nc.gpsimd.memset(page[2][:], 0.0)
+
+        msg = [keep.tile([P, J], F32, name="msg%d" % t) for t in range(PACK)]
+        gate = [keep.tile([P, J], F32, name="gate%d" % t) for t in range(PACK)]
+        turned = [keep.tile([P, PACK, P], F32, name="turned%d" % b, tag="turned%d" % b, align_bytes=64) for b in range(J // P)]
+        counts = {"edge": 0, "back": 1, "gate": 0}
+
+        def bank(kind, depth):
+            n = counts[kind]
+            counts.update({kind: n + 1})
+            return psum.tile([P, HALF], F32, name="%s_bank%d" % (kind, n), tag="%s%d" % (kind, n % depth))
+
+        def weighted_messages(h):
+            for i in range(HALF // P):
+                b = h * (HALF // P) + i
+                acc = bank("edge", 3)
+                nc.tensor.matmul_mx(
+                    out=acc[:],
+                    lhsT=src_w[h][:, i * P : (i + 1) * P].bitcast(FP8X4),
+                    lhsT_scale=src_s[:, b * P : (b + 1) * P],
+                    rhs=wc_w.bitcast(FP8X4),
+                    rhs_scale=wc_s,
+                    start=True,
+                    stop=True,
+                )
+                nc.scalar.activation(
+                    out=turned[b][:],
+                    in_=acc[:].rearrange("p (m t) -> p t m", t=PACK),
+                    func=ACT.Copy,
+                    scale=wgo_col[:, b : b + 1],
+                )
+
+        def slice_operands(t, h):
+            cols = slice(h * HALF, (h + 1) * HALF)
+            rows = slice(t * P, (t + 1) * P)
+            za = bank("gate", 2)
+            nc.tensor.matmul_mx(
+                out=za[:],
+                lhsT=wbd_w[:, rows].bitcast(FP8X4),
+                lhsT_scale=wbd_s[:, rows],
+                rhs=src_w[h][:].bitcast(FP8X4),
+                rhs_scale=src_s[:, cols],
+                start=True,
+                stop=False,
+            )
+            nc.tensor.matmul_mx(
+                out=za[:],
+                lhsT=wa_w[:, rows].bitcast(FP8X4),
+                lhsT_scale=wa_s[:, rows],
+                rhs=dst_w[h][:].bitcast(FP8X4),
+                rhs_scale=dst_s[h][:],
+                start=False,
+                stop=True,
+            )
+            back = bank("back", 3)
+            for i in range(HALF // P):
+                nc.tensor.transpose(back[:, i * P : (i + 1) * P], turned[h * (HALF // P) + i][:, t, :], ident[:])
+            nc.scalar.copy(out=msg[t][:, cols], in_=back[:])
+            nc.scalar.activation(out=gate[t][:, cols], in_=za[:], func=ACT.Sigmoid)
+
+        def scatter_half(t, h):
+            cols = slice(h * HALF, (h + 1) * HALF)
+            nc.vector.tensor_tensor(page[t][:].indirect(dst_list[:, half_cols[h]]), gate[t][:, cols], msg[t][:, cols], MULT)
+
+        weighted_messages(0)
+        slice_operands(0, 0)
+        slice_operands(1, 0)
+        weighted_messages(1)
+        slice_operands(0, 1)
+        slice_operands(1, 1)
+        for t in (2, 3):
+            slice_operands(t, 0)
+            slice_operands(t, 1)
+        page.append(keep.tile([P, T], F32, name="page3", tag="turned0", align_bytes=64))
+        nc.gpsimd.memset(page[3][:], 0.0)
+
+        out_rows = out_0.rearrange("(p t) c -> t p c", t=PACK)
+        pairs = [keep.tile([P, 2 * CHUNK * 2], BF16, name="pairs%d" % k, align_bytes=64) for k in range(CHUNKS)]
+
+        def pair_view(k, u):
+            return pairs[k][:].rearrange("p (u c e) -> p u c e", u=2, e=2)[:, u, :, :]
+
+        def page_cols(t, k):
+            return page[t][:, k * CHUNK : (k + 1) * CHUNK]
+
+        for h in range(2):
+            for t in range(2):
+                scatter_half(t, h)
+        for t in range(2):
+            nc.sync.dma_start(out=out_rows[t], in_=page[t][:])
+            for k in range(CHUNKS):
+                nc.scalar.copy(out=pair_view(k, 0)[:, :, t], in_=page_cols(t, k))
+        nc.vector.tensor_tensor(page[2][:].indirect(dst_list[:]), gate[2][:], msg[2][:], MULT)
+        nc.sync.dma_start(out=out_rows[2], in_=page[2][:])
+        for k in range(CHUNKS):
+            nc.scalar.copy(out=pair_view(k, 1), in_=page_cols(2, k).unsqueeze(2).to_broadcast([P, CHUNK, 2]))
+        nc.vector.tensor_tensor(page[3][:].indirect(dst_list[:]), gate[3][:], msg[3][:], MULT)
+        nc.sync.dma_start(out=out_rows[3], in_=page[3][:])
+
+        rounded = [keep.tile([P, CHUNK * PACK], BF16, name="rounded%d" % k, align_bytes=64) for k in range(CHUNKS)]
+        codes = [keep.tile([P, CHUNK], U32, name="codes%d" % k, align_bytes=64) for k in range(CHUNKS)]
+        out_s = keep.tile([P, T], U8, name="out_s", align_bytes=64)
+        out_words = words_of(out_1)
+
+        def merge_views(k):
+            return (
+                rounded[k][:].bitcast(F32).rearrange("p (c u) -> p c u", u=2),
+                pairs[k][:].bitcast(F32).rearrange("p (u c) -> p c u", u=2),
+            )
+
+        for k in (0, 1):
+            nc.vector.tensor_copy(out=pair_view(k, 1)[:, :, 1], in_=page_cols(3, k))
+        for k in (0, 1):
+            nc.vector.tensor_copy(*merge_views(k))
+        for k in (2, 3):
+            nc.scalar.copy(out=pair_view(k, 1)[:, :, 1], in_=page_cols(3, k))
+            nc.scalar.copy(*merge_views(k))
+        for k in range(CHUNKS):
+            cols = slice(k * CHUNK, (k + 1) * CHUNK)
+            nc.vector.quantize_mx(out=codes[k][:].bitcast(FP8X4), scales=out_s[:, cols], in_=rounded[k][:])
+            nc.sync.dma_start(out=out_words[:, cols], in_=codes[k][:].bitcast(I32))
+        for q in range(4):
+            queue = nc.sync if q % 2 == 0 else nc.scalar
+            queue.dma_start(out=out_2[0][4 * q : 4 * q + 4, :].bitcast(I32), in_=out_s[32 * q : 32 * q + 4, :].bitcast(I32))

@@ -20,6 +20,7 @@ P = 128
 PACK = 4
 HALF = J // 2
 LIST_COLS = J // 16
+BANK = 2048
 CHUNK = 512
 CHUNKS = T // CHUNK
 
@@ -39,94 +40,103 @@ def tile_list_rgg_noneP_kernel(
     nc = tc.nc
     with ExitStack() as ctx:
         keep = ctx.enter_context(tc.tile_pool(name="keep", bufs=1))
+        placed = ctx.enter_context(tc.tile_pool(name="placed", bufs=1))
         psum = ctx.enter_context(tc.psum_pool(name="psum", bufs=1))
 
         src_list = keep.tile([P, LIST_COLS], U16, name="src_list")
         dst_list = keep.tile([P, LIST_COLS], U16, name="dst_list")
-        tab_s = keep.tile([P, T], U8, name="tab_s", tag="page2_bytes", align_bytes=64)
-        tab_w = keep.tile([P, T], I32, name="tab_w", tag="page1_bytes", align_bytes=64)
-        wa_raw = keep.tile([P, PACK, N], F32, name="wa_raw")
-        w_scales = keep.tile([P, 2 * N], U8, name="w_scales", align_bytes=64)
+        tab_s = keep.tile([P, T], U8, name="tab_s", align_bytes=64)
+        zeros = placed.tile([P, 4992], F32, name="zeros", offset=7936, align_bytes=64)
         ident = keep.tile([P, P], F32, name="ident")
         wgo_rows = keep.tile([P, P], F32, name="wgo_rows")
 
         nc.vector.memset(tab_s[:].bitcast(I32), 0)
-        nc.sync.dma_start(out=src_list[:], in_=offs)
-        load_scale_rows(nc.sync, tab_s, tab_scales[0])
-        nc.sync.dma_start(out=dst_list[:], in_=offs2)
-        nc.sync.dma_start(out=wa_raw[:], in_=wa.rearrange("(p j) n -> p j n", j=PACK))
-        nc.sync.dma_start(out=tab_w[:], in_=words_of(tab_words))
-
-        nc.gpsimd.memset(wgo_rows[:], 0.0)
+        nc.vector.memset(zeros[:, 0:P], 0.0)
+        nc.vector.tensor_copy(out=wgo_rows[:], in_=zeros[:, 0:P])
         make_identity(nc, ident[:])
-        warm = keep.tile([P, 1], F32, name="warm", tag="w_words", align_bytes=64)
+        w_scales = placed.tile([P, 2 * N], U8, name="w_scales", offset=10240, align_bytes=64)
+        nc.gpsimd.memset(w_scales[:].bitcast(I32), 0)
+        page = [placed.tile([P, T], F32, name="page0", offset=15360, align_bytes=64)]
+        nc.gpsimd.memset(page[0][:], 0.0)
+        warm = keep.tile([P, 1], F32, name="warm")
         nc.scalar.activation(out=warm[:], in_=ident[:, 0:1], func=ACT.Sigmoid)
 
-        page = [keep.tile([P, T], F32, name="page%d" % t, align_bytes=64) for t in range(1)]
-        nc.vector.memset(page[0][:], 0.0)
-        nc.vector.memset(w_scales[:].bitcast(I32), 0)
-
-        w_words = keep.tile([P, 2 * N], I32, name="w_words", tag="w_words", align_bytes=64)
-        wc_w, wb_w = w_words[:, 0:N], w_words[:, N : 2 * N]
-        nc.sync.dma_start(out=wc_w, in_=words_of(wc_words))
-        load_scale_rows(nc.sync, w_scales[:, 0:N], wc_scales[0])
+        wa_raw = placed.tile([P, PACK, N], F32, name="wa_raw", offset=0, align_bytes=64)
+        wc_w = placed.tile([P, N], I32, name="wc_w", offset=8192, align_bytes=64)
+        wb_w = placed.tile([P, N], I32, name="wb_w", offset=12800, align_bytes=64)
+        tab_w = placed.tile([P, T], I32, name="tab_w", offset=27648, align_bytes=64)
+        nc.sync.dma_start(out=src_list[:], in_=offs)
+        nc.sync.dma_start(out=dst_list[:], in_=offs2)
+        load_scale_rows(nc.sync, tab_s, tab_scales[0])
+        nc.sync.dma_start(out=wa_raw[:], in_=wa.rearrange("(p j) n -> p j n", j=PACK))
+        nc.sync.dma_start(out=tab_w[:], in_=words_of(tab_words))
+        nc.sync.dma_start(out=wc_w[:], in_=words_of(wc_words))
+        nc.sync.dma_start(out=wb_w[:], in_=words_of(wb_words))
         nc.sync.dma_start(out=wgo_rows[0 : J // P, :], in_=wgo[0:1, :].rearrange("o (c p) -> (o c) p", p=P))
-        nc.sync.dma_start(out=wb_w, in_=words_of(wb_words))
+        load_scale_rows(nc.sync, w_scales[:, 0:N], wc_scales[0])
         load_scale_rows(nc.sync, w_scales[:, N : 2 * N], wb_scales[0])
         wc_s = w_scales[:, 0:N]
 
-        wa_bf = keep.tile([P, N * PACK], BF16, name="wa_bf", align_bytes=64)
+        wa_bf = placed.tile([P, N * PACK], BF16, name="wa_bf", offset=39936, align_bytes=64)
         nc.scalar.copy(
             out=wa_bf[:].rearrange("p (t m j) -> p m t j", t=PACK, j=PACK),
             in_=wa_raw[:].rearrange("p j (m t) -> p m t j", t=PACK),
         )
 
-        wgo_bank = psum.tile([P, HALF], F32, name="wgo_bank", tag="back0")
+        wgo_bank = psum.tile([P, HALF], F32, name="wgo_bank", offset=7 * BANK)
         nc.tensor.transpose(wgo_bank[:, 0:P], wgo_rows[:], ident[:])
         wgo_col = keep.tile([P, J // P], F32, name="wgo_col")
         nc.scalar.copy(out=wgo_col[:], in_=wgo_bank[:, 0 : J // P])
 
         src_s = keep.tile([P, J], U8, name="src_s", align_bytes=64)
-        src_w = [keep.tile([P, HALF], U32, name="src_w%d" % h, align_bytes=64) for h in range(2)]
-        dst_s = [keep.tile([P, HALF], U8, name="dst_s%d" % h, align_bytes=64) for h in range(2)]
-        dst_w = [keep.tile([P, HALF], U32, name="dst_w%d" % h, align_bytes=64) for h in range(2)]
+        dst_s = keep.tile([P, J], U8, name="dst_s", align_bytes=64)
+        src_w = [
+            keep.tile([P, HALF], U32, name="src_w0", align_bytes=64),
+            placed.tile([P, HALF], U32, name="src_w1", offset=11264, align_bytes=64),
+        ]
+        dst_w = [
+            keep.tile([P, HALF], U32, name="dst_w0", align_bytes=64),
+            placed.tile([P, HALF], U32, name="dst_w1", offset=13312, align_bytes=64),
+        ]
         half_cols = [slice(h * LIST_COLS // 2, (h + 1) * LIST_COLS // 2) for h in range(2)]
         tab_u = tab_w[:].bitcast(U32)
 
         nc.vector.tensor_copy(src_s[:], tab_s[:].indirect(src_list[:]))
-        nc.vector.tensor_copy(dst_s[0][:], tab_s[:].indirect(dst_list[:, half_cols[0]]))
+        nc.vector.tensor_copy(dst_s[:], tab_s[:].indirect(dst_list[:]))
         nc.vector.tensor_copy(src_w[0][:], tab_u.indirect(src_list[:, half_cols[0]]))
         nc.vector.tensor_copy(dst_w[0][:], tab_u.indirect(dst_list[:, half_cols[0]]))
 
         wa_w = keep.tile([P, N], U32, name="wa_w", align_bytes=64)
         wa_s = keep.tile([P, N], U8, name="wa_s", align_bytes=64)
         nc.vector.quantize_mx(out=wa_w[:].bitcast(FP8X4), scales=wa_s[:], in_=wa_bf[:])
-        wbd_w = keep.tile([P, N], I32, name="wbd_w", align_bytes=64)
-        wbd_s = keep.tile([P, N], U8, name="wbd_s", align_bytes=64)
-        nc.vector.tensor_copy(out=wbd_w[:].rearrange("p (t m) -> p t m", t=PACK), in_=wb_w.rearrange("p (m t) -> p t m", t=PACK))
+
+        wbd_w = placed.tile([P, N], I32, name="wbd_w", offset=39936, align_bytes=64)
+        wbd_s = placed.tile([P, N], U8, name="wbd_s", offset=41984, align_bytes=64)
         nc.vector.tensor_copy(
             out=wbd_s[:].rearrange("p (t m) -> p t m", t=PACK),
             in_=w_scales[:, N : 2 * N].rearrange("p (m t) -> p t m", t=PACK),
         )
 
+        nc.vector.tensor_copy(out=wbd_w[:].rearrange("p (t m) -> p t m", t=PACK), in_=wb_w[:].rearrange("p (m t) -> p t m", t=PACK))
         nc.vector.tensor_copy(src_w[1][:], tab_u.indirect(src_list[:, half_cols[1]]))
         nc.vector.tensor_copy(dst_w[1][:], tab_u.indirect(dst_list[:, half_cols[1]]))
-        nc.vector.tensor_copy(dst_s[1][:], tab_s[:].indirect(dst_list[:, half_cols[1]]))
 
-        page.append(keep.tile([P, T], F32, name="page1", tag="page1_bytes", align_bytes=64))
-        page.append(keep.tile([P, T], F32, name="page2", tag="page2_bytes", align_bytes=64))
+        page.append(placed.tile([P, T], F32, name="page1", offset=23552, align_bytes=64))
+        page.append(placed.tile([P, T], F32, name="page2", offset=31744, align_bytes=64))
         nc.gpsimd.memset(page[1][:], 0.0)
         nc.gpsimd.memset(page[2][:], 0.0)
 
         msg = [keep.tile([P, J], F32, name="msg%d" % t) for t in range(PACK)]
         gate = [keep.tile([P, J], F32, name="gate%d" % t) for t in range(PACK)]
         turned = [keep.tile([P, PACK, P], F32, name="turned%d" % b, tag="turned%d" % b, align_bytes=64) for b in range(J // P)]
-        counts = {"edge": 0, "back": 1, "gate": 0}
+        counts = {"edge": 0, "back": 0, "gate": 0}
+
+        first_bank = {"edge": 0, "back": 3, "gate": 5}
 
         def bank(kind, depth):
             n = counts[kind]
             counts.update({kind: n + 1})
-            return psum.tile([P, HALF], F32, name="%s_bank%d" % (kind, n), tag="%s%d" % (kind, n % depth))
+            return psum.tile([P, HALF], F32, name="%s_bank%d" % (kind, n), offset=(first_bank[kind] + n % depth) * BANK)
 
         def weighted_messages(h):
             for i in range(HALF // P):
@@ -136,7 +146,7 @@ def tile_list_rgg_noneP_kernel(
                     out=acc[:],
                     lhsT=src_w[h][:, i * P : (i + 1) * P].bitcast(FP8X4),
                     lhsT_scale=src_s[:, b * P : (b + 1) * P],
-                    rhs=wc_w.bitcast(FP8X4),
+                    rhs=wc_w[:].bitcast(FP8X4),
                     rhs_scale=wc_s,
                     start=True,
                     stop=True,
@@ -166,11 +176,11 @@ def tile_list_rgg_noneP_kernel(
                 lhsT=wa_w[:, rows].bitcast(FP8X4),
                 lhsT_scale=wa_s[:, rows],
                 rhs=dst_w[h][:].bitcast(FP8X4),
-                rhs_scale=dst_s[h][:],
+                rhs_scale=dst_s[:, cols],
                 start=False,
                 stop=True,
             )
-            back = bank("back", 3)
+            back = bank("back", 2)
             for i in range(HALF // P):
                 nc.tensor.transpose(back[:, i * P : (i + 1) * P], turned[h * (HALF // P) + i][:, t, :], ident[:])
             nc.scalar.copy(out=msg[t][:, cols], in_=back[:])

@@ -46,7 +46,7 @@ def tile_list_rgg_noneP_kernel(
         src_list = keep.tile([P, LIST_COLS], U16, name="src_list")
         dst_list = keep.tile([P, LIST_COLS], U16, name="dst_list")
         tab_s = keep.tile([P, T], U8, name="tab_s", align_bytes=64)
-        zeros = placed.tile([P, 4992], F32, name="zeros", offset=7936, align_bytes=64)
+        zeros = placed.tile([P, 5376], F32, name="zeros", offset=7936, align_bytes=64)
         ident = keep.tile([P, P], F32, name="ident")
         wgo_rows = keep.tile([P, P], F32, name="wgo_rows")
 
@@ -54,17 +54,19 @@ def tile_list_rgg_noneP_kernel(
         nc.vector.memset(zeros[:, 0:P], 0.0)
         nc.vector.tensor_copy(out=wgo_rows[:], in_=zeros[:, 0:P])
         make_identity(nc, ident[:])
-        w_scales = placed.tile([P, 2 * N], U8, name="w_scales", offset=10240, align_bytes=64)
-        nc.gpsimd.memset(w_scales[:].bitcast(I32), 0)
-        page = [placed.tile([P, T], F32, name="page0", offset=15360, align_bytes=64)]
+        wc_s = placed.tile([P, N], U8, name="wc_s", offset=10240, align_bytes=64)
+        wb_s = placed.tile([P, N], U8, name="wb_s", offset=14592, align_bytes=64)
+        nc.gpsimd.memset(wc_s[:].bitcast(I32), 0)
+        nc.gpsimd.memset(wb_s[:].bitcast(I32), 0)
+        page = [placed.tile([P, T], F32, name="page0", offset=16896, align_bytes=64)]
         nc.gpsimd.memset(page[0][:], 0.0)
         warm = keep.tile([P, 1], F32, name="warm")
         nc.scalar.activation(out=warm[:], in_=ident[:, 0:1], func=ACT.Sigmoid)
 
         wa_raw = placed.tile([P, PACK, N], F32, name="wa_raw", offset=0, align_bytes=64)
         wc_w = placed.tile([P, N], I32, name="wc_w", offset=8192, align_bytes=64)
-        wb_w = placed.tile([P, N], I32, name="wb_w", offset=12800, align_bytes=64)
-        tab_w = placed.tile([P, T], I32, name="tab_w", offset=27648, align_bytes=64)
+        wb_w = placed.tile([P, N], I32, name="wb_w", offset=10752, align_bytes=64)
+        tab_w = placed.tile([P, T], I32, name="tab_w", offset=29184, align_bytes=64)
         nc.sync.dma_start(out=src_list[:], in_=offs)
         nc.sync.dma_start(out=dst_list[:], in_=offs2)
         load_scale_rows(nc.sync, tab_s, tab_scales[0])
@@ -73,11 +75,10 @@ def tile_list_rgg_noneP_kernel(
         nc.sync.dma_start(out=wc_w[:], in_=words_of(wc_words))
         nc.sync.dma_start(out=wb_w[:], in_=words_of(wb_words))
         nc.sync.dma_start(out=wgo_rows[0 : J // P, :], in_=wgo[0:1, :].rearrange("o (c p) -> (o c) p", p=P))
-        load_scale_rows(nc.sync, w_scales[:, 0:N], wc_scales[0])
-        load_scale_rows(nc.sync, w_scales[:, N : 2 * N], wb_scales[0])
-        wc_s = w_scales[:, 0:N]
+        load_scale_rows(nc.sync, wc_s, wc_scales[0])
+        load_scale_rows(nc.sync, wb_s, wb_scales[0])
 
-        wa_bf = placed.tile([P, N * PACK], BF16, name="wa_bf", offset=39936, align_bytes=64)
+        wa_bf = placed.tile([P, N * PACK], BF16, name="wa_bf", offset=41472, align_bytes=64)
         nc.scalar.copy(
             out=wa_bf[:].rearrange("p (t m j) -> p m t j", t=PACK, j=PACK),
             in_=wa_raw[:].rearrange("p j (m t) -> p m t j", t=PACK),
@@ -92,11 +93,11 @@ def tile_list_rgg_noneP_kernel(
         dst_s = keep.tile([P, J], U8, name="dst_s", align_bytes=64)
         src_w = [
             keep.tile([P, HALF], U32, name="src_w0", align_bytes=64),
-            placed.tile([P, HALF], U32, name="src_w1", offset=11264, align_bytes=64),
+            placed.tile([P, HALF], U32, name="src_w1", offset=12800, align_bytes=64),
         ]
         dst_w = [
             keep.tile([P, HALF], U32, name="dst_w0", align_bytes=64),
-            placed.tile([P, HALF], U32, name="dst_w1", offset=13312, align_bytes=64),
+            placed.tile([P, HALF], U32, name="dst_w1", offset=14848, align_bytes=64),
         ]
         half_cols = [slice(h * LIST_COLS // 2, (h + 1) * LIST_COLS // 2) for h in range(2)]
         tab_u = tab_w[:].bitcast(U32)
@@ -110,19 +111,19 @@ def tile_list_rgg_noneP_kernel(
         wa_s = keep.tile([P, N], U8, name="wa_s", align_bytes=64)
         nc.vector.quantize_mx(out=wa_w[:].bitcast(FP8X4), scales=wa_s[:], in_=wa_bf[:])
 
-        wbd_w = placed.tile([P, N], I32, name="wbd_w", offset=39936, align_bytes=64)
-        wbd_s = placed.tile([P, N], U8, name="wbd_s", offset=41984, align_bytes=64)
+        wbd_w = placed.tile([P, N], I32, name="wbd_w", offset=41472, align_bytes=64)
+        wbd_s = placed.tile([P, N], U8, name="wbd_s", offset=43520, align_bytes=64)
+        nc.vector.tensor_copy(out=wbd_w[:].rearrange("p (t m) -> p t m", t=PACK), in_=wb_w[:].rearrange("p (m t) -> p t m", t=PACK))
         nc.vector.tensor_copy(
             out=wbd_s[:].rearrange("p (t m) -> p t m", t=PACK),
-            in_=w_scales[:, N : 2 * N].rearrange("p (m t) -> p t m", t=PACK),
+            in_=wb_s[:].rearrange("p (m t) -> p t m", t=PACK),
         )
 
-        nc.vector.tensor_copy(out=wbd_w[:].rearrange("p (t m) -> p t m", t=PACK), in_=wb_w[:].rearrange("p (m t) -> p t m", t=PACK))
         nc.vector.tensor_copy(src_w[1][:], tab_u.indirect(src_list[:, half_cols[1]]))
         nc.vector.tensor_copy(dst_w[1][:], tab_u.indirect(dst_list[:, half_cols[1]]))
 
-        page.append(placed.tile([P, T], F32, name="page1", offset=23552, align_bytes=64))
-        page.append(placed.tile([P, T], F32, name="page2", offset=31744, align_bytes=64))
+        page.append(placed.tile([P, T], F32, name="page1", offset=25088, align_bytes=64))
+        page.append(placed.tile([P, T], F32, name="page2", offset=33280, align_bytes=64))
         nc.gpsimd.memset(page[1][:], 0.0)
         nc.gpsimd.memset(page[2][:], 0.0)
 
@@ -147,7 +148,7 @@ def tile_list_rgg_noneP_kernel(
                     lhsT=src_w[h][:, i * P : (i + 1) * P].bitcast(FP8X4),
                     lhsT_scale=src_s[:, b * P : (b + 1) * P],
                     rhs=wc_w[:].bitcast(FP8X4),
-                    rhs_scale=wc_s,
+                    rhs_scale=wc_s[:],
                     start=True,
                     stop=True,
                 )

@@ -46,43 +46,55 @@ def tile_list_rgg_noneP_kernel(
         src_list = keep.tile([P, LIST_COLS], U16, name="src_list")
         dst_list = keep.tile([P, LIST_COLS], U16, name="dst_list")
         tab_s = keep.tile([P, T], U8, name="tab_s", align_bytes=64)
-        zeros = placed.tile([P, 5376], F32, name="zeros", offset=7936, align_bytes=64)
+        zeros_a = placed.tile([P, 1152], F32, name="zeros_a", offset=37120, align_bytes=64)
+        zeros = placed.tile([P, 2320], I32, name="zeros", offset=8192, align_bytes=64)
+        wc_s = keep.tile([P, N], U8, name="wc_s", align_bytes=64)
         ident = keep.tile([P, P], F32, name="ident")
         wgo_rows = keep.tile([P, P], F32, name="wgo_rows")
 
-        nc.vector.memset(tab_s[:].bitcast(I32), 0)
-        nc.vector.memset(zeros[:, 0:P], 0.0)
-        nc.vector.tensor_copy(out=wgo_rows[:], in_=zeros[:, 0:P])
-        make_identity(nc, ident[:])
-        wc_s = placed.tile([P, N], U8, name="wc_s", offset=10240, align_bytes=64)
-        wb_s = placed.tile([P, N], U8, name="wb_s", offset=14592, align_bytes=64)
-        nc.gpsimd.memset(wc_s[:].bitcast(I32), 0)
-        nc.gpsimd.memset(wb_s[:].bitcast(I32), 0)
-        page = [placed.tile([P, T], F32, name="page0", offset=16896, align_bytes=64)]
-        nc.gpsimd.memset(page[0][:], 0.0)
+        warm_in = keep.tile([P, 1], F32, name="warm_in")
         warm = keep.tile([P, 1], F32, name="warm")
-        nc.scalar.activation(out=warm[:], in_=ident[:, 0:1], func=ACT.Sigmoid)
+        nc.vector.memset(warm_in[:], 0.0)
+        nc.scalar.activation(out=warm[:], in_=warm_in[:], func=ACT.Sigmoid)
+        nc.gpsimd.memset(tab_s[:].bitcast(I32), 0)
+        nc.gpsimd.memset(zeros_a[:, 0:P], 0.0)
+        nc.gpsimd.memset(zeros[:, 0:P], 0)
+        nc.vector.tensor_copy(out=wgo_rows[:], in_=zeros_a[:, 0:P])
+        nc.vector.tensor_copy(out=wc_s[:].bitcast(I32), in_=zeros[:, 0:P])
+        make_identity(nc, ident[:])
+        wb_s_room = placed.tile([P, 2 * N], U8, name="wb_s_room", offset=14592, align_bytes=64)
+        wb_s = wb_s_room[:, 0:N]
+        nc.vector.memset(wb_s.bitcast(I32), 0)
+        page = [placed.tile([P, T], F32, name="page0", offset=17408, align_bytes=64)]
+        nc.gpsimd.memset(page[0][:], 0.0)
 
-        wa_raw = placed.tile([P, PACK, N], F32, name="wa_raw", offset=0, align_bytes=64)
+        wa_raw = [
+            placed.tile([P, PACK, N // 2], F32, name="wa_raw%d" % c, offset=37376 + 4096 * c, align_bytes=64) for c in range(2)
+        ]
         wc_w = placed.tile([P, N], I32, name="wc_w", offset=8192, align_bytes=64)
         wb_w = placed.tile([P, N], I32, name="wb_w", offset=10752, align_bytes=64)
         tab_w = placed.tile([P, T], I32, name="tab_w", offset=29184, align_bytes=64)
         nc.sync.dma_start(out=src_list[:], in_=offs)
         nc.sync.dma_start(out=dst_list[:], in_=offs2)
         load_scale_rows(nc.sync, tab_s, tab_scales[0])
-        nc.sync.dma_start(out=wa_raw[:], in_=wa.rearrange("(p j) n -> p j n", j=PACK))
+        nc.sync.dma_start(out=wgo_rows[0 : J // P, :], in_=wgo[0:1, :].rearrange("o (c p) -> (o c) p", p=P))
         nc.sync.dma_start(out=tab_w[:], in_=words_of(tab_words))
+        wa_rows = wa.rearrange("(p j) n -> p j n", j=PACK)
+        for c in range(2):
+            nc.sync.dma_start(out=wa_raw[c][:], in_=wa_rows[:, :, c * N // 2 : (c + 1) * N // 2])
+        load_scale_rows(nc.sync, wc_s, wc_scales[0])
         nc.sync.dma_start(out=wc_w[:], in_=words_of(wc_words))
         nc.sync.dma_start(out=wb_w[:], in_=words_of(wb_words))
-        nc.sync.dma_start(out=wgo_rows[0 : J // P, :], in_=wgo[0:1, :].rearrange("o (c p) -> (o c) p", p=P))
-        load_scale_rows(nc.sync, wc_s, wc_scales[0])
         load_scale_rows(nc.sync, wb_s, wb_scales[0])
 
-        wa_bf = placed.tile([P, N * PACK], BF16, name="wa_bf", offset=41472, align_bytes=64)
-        nc.scalar.copy(
-            out=wa_bf[:].rearrange("p (t m j) -> p m t j", t=PACK, j=PACK),
-            in_=wa_raw[:].rearrange("p j (m t) -> p m t j", t=PACK),
-        )
+        wa_w = keep.tile([P, N], U32, name="wa_w", align_bytes=64)
+        wa_s = keep.tile([P, N], U8, name="wa_s", align_bytes=64)
+        wa_bf = keep.tile([P, N * PACK], BF16, name="wa_bf", align_bytes=64)
+        for c in range(2):
+            nc.scalar.copy(
+                out=wa_bf[:].rearrange("p (t m j) -> p m t j", t=PACK, j=PACK)[:, c * P // 2 : (c + 1) * P // 2, :, :],
+                in_=wa_raw[c][:].rearrange("p j (m t) -> p m t j", t=PACK),
+            )
 
         wgo_bank = psum.tile([P, HALF], F32, name="wgo_bank", offset=7 * BANK)
         nc.tensor.transpose(wgo_bank[:, 0:P], wgo_rows[:], ident[:])
@@ -90,61 +102,60 @@ def tile_list_rgg_noneP_kernel(
         nc.scalar.copy(out=wgo_col[:], in_=wgo_bank[:, 0 : J // P])
 
         src_s = keep.tile([P, J], U8, name="src_s", align_bytes=64)
-        dst_s = keep.tile([P, J], U8, name="dst_s", align_bytes=64)
+        dst_s = [
+            keep.tile([P, HALF], U8, name="dst_s0", align_bytes=64),
+            placed.tile([P, HALF], U8, name="dst_s1", offset=14848, align_bytes=64),
+        ]
         src_w = [
             keep.tile([P, HALF], U32, name="src_w0", align_bytes=64),
             placed.tile([P, HALF], U32, name="src_w1", offset=12800, align_bytes=64),
         ]
         dst_w = [
             keep.tile([P, HALF], U32, name="dst_w0", align_bytes=64),
-            placed.tile([P, HALF], U32, name="dst_w1", offset=14848, align_bytes=64),
+            placed.tile([P, HALF], U32, name="dst_w1", offset=15360, align_bytes=64),
         ]
         half_cols = [slice(h * LIST_COLS // 2, (h + 1) * LIST_COLS // 2) for h in range(2)]
         tab_u = tab_w[:].bitcast(U32)
 
         nc.vector.tensor_copy(src_s[:], tab_s[:].indirect(src_list[:]))
-        nc.vector.tensor_copy(dst_s[:], tab_s[:].indirect(dst_list[:]))
+        nc.vector.tensor_copy(dst_s[0][:], tab_s[:].indirect(dst_list[:, half_cols[0]]))
         nc.vector.tensor_copy(src_w[0][:], tab_u.indirect(src_list[:, half_cols[0]]))
         nc.vector.tensor_copy(dst_w[0][:], tab_u.indirect(dst_list[:, half_cols[0]]))
 
-        wa_w = keep.tile([P, N], U32, name="wa_w", align_bytes=64)
-        wa_s = keep.tile([P, N], U8, name="wa_s", align_bytes=64)
         nc.vector.quantize_mx(out=wa_w[:].bitcast(FP8X4), scales=wa_s[:], in_=wa_bf[:])
-
-        wbd_w = placed.tile([P, N], I32, name="wbd_w", offset=41472, align_bytes=64)
-        wbd_s = placed.tile([P, N], U8, name="wbd_s", offset=43520, align_bytes=64)
+        wbd_w = keep.tile([P, N], I32, name="wbd_w", align_bytes=64)
+        wbd_s = keep.tile([P, N], U8, name="wbd_s", align_bytes=64)
         nc.vector.tensor_copy(out=wbd_w[:].rearrange("p (t m) -> p t m", t=PACK), in_=wb_w[:].rearrange("p (m t) -> p t m", t=PACK))
         nc.vector.tensor_copy(
             out=wbd_s[:].rearrange("p (t m) -> p t m", t=PACK),
-            in_=wb_s[:].rearrange("p (m t) -> p t m", t=PACK),
+            in_=wb_s.rearrange("p (m t) -> p t m", t=PACK),
         )
 
         nc.vector.tensor_copy(src_w[1][:], tab_u.indirect(src_list[:, half_cols[1]]))
+        nc.vector.tensor_copy(dst_s[1][:], tab_s[:].indirect(dst_list[:, half_cols[1]]))
         nc.vector.tensor_copy(dst_w[1][:], tab_u.indirect(dst_list[:, half_cols[1]]))
 
-        page.append(placed.tile([P, T], F32, name="page1", offset=25088, align_bytes=64))
-        page.append(placed.tile([P, T], F32, name="page2", offset=33280, align_bytes=64))
+        page.append(placed.tile([P, T], F32, name="page1", offset=25600, align_bytes=64))
+        page.append(placed.tile([P, T], F32, name="page2", offset=33792, align_bytes=64))
         nc.gpsimd.memset(page[1][:], 0.0)
         nc.gpsimd.memset(page[2][:], 0.0)
 
         msg = [keep.tile([P, J], F32, name="msg%d" % t) for t in range(PACK)]
         gate = [keep.tile([P, J], F32, name="gate%d" % t) for t in range(PACK)]
         turned = [keep.tile([P, PACK, P], F32, name="turned%d" % b, tag="turned%d" % b, align_bytes=64) for b in range(J // P)]
-        counts = {"edge": 0, "back": 0, "gate": 0}
+        made = []
 
-        first_bank = {"edge": 0, "back": 3, "gate": 5}
+        def banks(first, count):
+            acc = psum.tile([P, count, HALF], F32, name="acc%d" % len(made), offset=first * BANK)
+            made.append(acc)
+            return [acc[:, i, :] for i in range(count)]
 
-        def bank(kind, depth):
-            n = counts[kind]
-            counts.update({kind: n + 1})
-            return psum.tile([P, HALF], F32, name="%s_bank%d" % (kind, n), offset=(first_bank[kind] + n % depth) * BANK)
-
-        def weighted_messages(h):
+        def weighted_messages(h, accs):
             for i in range(HALF // P):
                 b = h * (HALF // P) + i
-                acc = bank("edge", 3)
+                acc = accs[i]
                 nc.tensor.matmul_mx(
-                    out=acc[:],
+                    out=acc,
                     lhsT=src_w[h][:, i * P : (i + 1) * P].bitcast(FP8X4),
                     lhsT_scale=src_s[:, b * P : (b + 1) * P],
                     rhs=wc_w[:].bitcast(FP8X4),
@@ -154,17 +165,18 @@ def tile_list_rgg_noneP_kernel(
                 )
                 nc.scalar.activation(
                     out=turned[b][:],
-                    in_=acc[:].rearrange("p (m t) -> p t m", t=PACK),
+                    in_=acc.rearrange("p (m t) -> p t m", t=PACK),
                     func=ACT.Copy,
                     scale=wgo_col[:, b : b + 1],
                 )
 
-        def slice_operands(t, h):
+        def slice_operands(t, h, back, za):
             cols = slice(h * HALF, (h + 1) * HALF)
             rows = slice(t * P, (t + 1) * P)
-            za = bank("gate", 2)
+            for i in range(HALF // P):
+                nc.tensor.transpose(back[:, i * P : (i + 1) * P], turned[h * (HALF // P) + i][:, t, :], ident[:])
             nc.tensor.matmul_mx(
-                out=za[:],
+                out=za,
                 lhsT=wbd_w[:, rows].bitcast(FP8X4),
                 lhsT_scale=wbd_s[:, rows],
                 rhs=src_w[h][:].bitcast(FP8X4),
@@ -173,33 +185,27 @@ def tile_list_rgg_noneP_kernel(
                 stop=False,
             )
             nc.tensor.matmul_mx(
-                out=za[:],
+                out=za,
                 lhsT=wa_w[:, rows].bitcast(FP8X4),
                 lhsT_scale=wa_s[:, rows],
                 rhs=dst_w[h][:].bitcast(FP8X4),
-                rhs_scale=dst_s[:, cols],
+                rhs_scale=dst_s[h][:],
                 start=False,
                 stop=True,
             )
-            back = bank("back", 2)
-            for i in range(HALF // P):
-                nc.tensor.transpose(back[:, i * P : (i + 1) * P], turned[h * (HALF // P) + i][:, t, :], ident[:])
-            nc.scalar.copy(out=msg[t][:, cols], in_=back[:])
-            nc.scalar.activation(out=gate[t][:, cols], in_=za[:], func=ACT.Sigmoid)
+            nc.scalar.activation(out=gate[t][:, cols], in_=za, func=ACT.Sigmoid)
+            nc.scalar.copy(out=msg[t][:, cols], in_=back)
 
         def scatter_half(t, h):
             cols = slice(h * HALF, (h + 1) * HALF)
             nc.vector.tensor_tensor(page[t][:].indirect(dst_list[:, half_cols[h]]), gate[t][:, cols], msg[t][:, cols], MULT)
 
-        weighted_messages(0)
-        slice_operands(0, 0)
-        slice_operands(1, 0)
-        weighted_messages(1)
-        slice_operands(0, 1)
-        slice_operands(1, 1)
-        for t in (2, 3):
-            slice_operands(t, 0)
-            slice_operands(t, 1)
+        weighted_messages(0, [banks(i, 1)[0] for i in range(4)])
+        slice_operands(0, 0, banks(4, 4)[0], banks(2, 1)[0])
+        slice_operands(1, 0, banks(3, 1)[0], banks(2, 1)[0])
+        weighted_messages(1, [banks(4 + i, 1)[0] for i in range(4)])
+        for t, h, back, za in ((0, 1, 0, 2), (1, 1, 1, 3), (2, 0, 4, 5), (2, 1, 6, 7), (3, 0, 0, 2), (3, 1, 1, 3)):
+            slice_operands(t, h, banks(back, 1)[0], banks(za, 1)[0])
         page.append(keep.tile([P, T], F32, name="page3", tag="turned0", align_bytes=64))
         nc.gpsimd.memset(page[3][:], 0.0)
 

@@ -46,25 +46,25 @@ def tile_list_rgg_noneP_kernel(
         src_list = keep.tile([P, LIST_COLS], U16, name="src_list")
         dst_list = keep.tile([P, LIST_COLS], U16, name="dst_list")
         tab_s = keep.tile([P, T], U8, name="tab_s", align_bytes=64)
-        zeros_a = placed.tile([P, 1152], F32, name="zeros_a", offset=37120, align_bytes=64)
-        zeros = placed.tile([P, 2320], I32, name="zeros", offset=8192, align_bytes=64)
+        zeros_a = placed.tile([P, P], F32, name="zeros_a", offset=53760, align_bytes=64)
+        zeros = placed.tile([P, 8512], I32, name="zeros", offset=8192, align_bytes=64)
         wc_s = keep.tile([P, N], U8, name="wc_s", align_bytes=64)
         ident = keep.tile([P, P], F32, name="ident")
         wgo_rows = keep.tile([P, P], F32, name="wgo_rows")
 
         warm_in = keep.tile([P, 1], F32, name="warm_in")
         warm = keep.tile([P, 1], F32, name="warm")
+        nc.vector.memset(tab_s[:].bitcast(I32), 0)
+        nc.vector.memset(zeros_a[:, 0:P], 0.0)
+        nc.vector.memset(zeros[:, 0:P], 0)
         nc.vector.memset(warm_in[:], 0.0)
         nc.scalar.activation(out=warm[:], in_=warm_in[:], func=ACT.Sigmoid)
-        nc.gpsimd.memset(tab_s[:].bitcast(I32), 0)
-        nc.gpsimd.memset(zeros_a[:, 0:P], 0.0)
-        nc.gpsimd.memset(zeros[:, 0:P], 0)
         nc.vector.tensor_copy(out=wgo_rows[:], in_=zeros_a[:, 0:P])
         nc.vector.tensor_copy(out=wc_s[:].bitcast(I32), in_=zeros[:, 0:P])
         make_identity(nc, ident[:])
         wb_s_room = placed.tile([P, 2 * N], U8, name="wb_s_room", offset=14592, align_bytes=64)
         wb_s = wb_s_room[:, 0:N]
-        nc.vector.memset(wb_s.bitcast(I32), 0)
+        nc.gpsimd.memset(wb_s.bitcast(I32), 0)
         page = [placed.tile([P, T], F32, name="page0", offset=17408, align_bytes=64)]
         nc.gpsimd.memset(page[0][:], 0.0)
 
@@ -73,16 +73,16 @@ def tile_list_rgg_noneP_kernel(
         ]
         wc_w = placed.tile([P, N], I32, name="wc_w", offset=8192, align_bytes=64)
         wb_w = placed.tile([P, N], I32, name="wb_w", offset=10752, align_bytes=64)
-        tab_w = placed.tile([P, T], I32, name="tab_w", offset=29184, align_bytes=64)
+        tab_w = placed.tile([P, T], I32, name="tab_w", offset=53760, align_bytes=64)
         nc.sync.dma_start(out=src_list[:], in_=offs)
         nc.sync.dma_start(out=dst_list[:], in_=offs2)
         load_scale_rows(nc.sync, tab_s, tab_scales[0])
         nc.sync.dma_start(out=wgo_rows[0 : J // P, :], in_=wgo[0:1, :].rearrange("o (c p) -> (o c) p", p=P))
         nc.sync.dma_start(out=tab_w[:], in_=words_of(tab_words))
+        load_scale_rows(nc.sync, wc_s, wc_scales[0])
         wa_rows = wa.rearrange("(p j) n -> p j n", j=PACK)
         for c in range(2):
             nc.sync.dma_start(out=wa_raw[c][:], in_=wa_rows[:, :, c * N // 2 : (c + 1) * N // 2])
-        load_scale_rows(nc.sync, wc_s, wc_scales[0])
         nc.sync.dma_start(out=wc_w[:], in_=words_of(wc_words))
         nc.sync.dma_start(out=wb_w[:], in_=words_of(wb_words))
         load_scale_rows(nc.sync, wb_s, wb_scales[0])
@@ -135,14 +135,14 @@ def tile_list_rgg_noneP_kernel(
         nc.vector.tensor_copy(dst_s[1][:], tab_s[:].indirect(dst_list[:, half_cols[1]]))
         nc.vector.tensor_copy(dst_w[1][:], tab_u.indirect(dst_list[:, half_cols[1]]))
 
-        page.append(placed.tile([P, T], F32, name="page1", offset=25600, align_bytes=64))
-        page.append(placed.tile([P, T], F32, name="page2", offset=33792, align_bytes=64))
+        page.append(placed.tile([P, T], F32, name="page1", offset=49664, align_bytes=64))
+        page.append(placed.tile([P, T], F32, name="page2", offset=57856, align_bytes=64))
         nc.gpsimd.memset(page[1][:], 0.0)
         nc.gpsimd.memset(page[2][:], 0.0)
 
         msg = [keep.tile([P, J], F32, name="msg%d" % t) for t in range(PACK)]
         gate = [keep.tile([P, J], F32, name="gate%d" % t) for t in range(PACK)]
-        turned = [keep.tile([P, PACK, P], F32, name="turned%d" % b, tag="turned%d" % b, align_bytes=64) for b in range(J // P)]
+        turned = [keep.tile([P, PACK, P], F32, name="turned%d" % b, align_bytes=64) for b in range(J // P)]
         made = []
 
         def banks(first, count):
@@ -206,8 +206,7 @@ def tile_list_rgg_noneP_kernel(
         weighted_messages(1, [banks(4 + i, 1)[0] for i in range(4)])
         for t, h, back, za in ((0, 1, 0, 2), (1, 1, 1, 3), (2, 0, 4, 5), (2, 1, 6, 7), (3, 0, 0, 2), (3, 1, 1, 3)):
             slice_operands(t, h, banks(back, 1)[0], banks(za, 1)[0])
-        page.append(keep.tile([P, T], F32, name="page3", tag="turned0", align_bytes=64))
-        nc.gpsimd.memset(page[3][:], 0.0)
+        page.append(page[0])
 
         out_rows = out_0.rearrange("(p t) c -> t p c", t=PACK)
         pairs = [keep.tile([P, 2 * CHUNK * 2], BF16, name="pairs%d" % k, align_bytes=64) for k in range(CHUNKS)]
@@ -218,24 +217,13 @@ def tile_list_rgg_noneP_kernel(
         def page_cols(t, k):
             return page[t][:, k * CHUNK : (k + 1) * CHUNK]
 
-        for h in range(2):
-            for t in range(2):
-                scatter_half(t, h)
-        for t in range(2):
-            nc.sync.dma_start(out=out_rows[t], in_=page[t][:])
-            for k in range(CHUNKS):
-                nc.scalar.copy(out=pair_view(k, 0)[:, :, t], in_=page_cols(t, k))
-        nc.vector.tensor_tensor(page[2][:].indirect(dst_list[:]), gate[2][:], msg[2][:], MULT)
-        nc.sync.dma_start(out=out_rows[2], in_=page[2][:])
-        for k in range(CHUNKS):
-            nc.scalar.copy(out=pair_view(k, 1), in_=page_cols(2, k).unsqueeze(2).to_broadcast([P, CHUNK, 2]))
-        nc.vector.tensor_tensor(page[3][:].indirect(dst_list[:]), gate[3][:], msg[3][:], MULT)
-        nc.sync.dma_start(out=out_rows[3], in_=page[3][:])
-
         rounded = [keep.tile([P, CHUNK * PACK], BF16, name="rounded%d" % k, align_bytes=64) for k in range(CHUNKS)]
         codes = [keep.tile([P, CHUNK], U32, name="codes%d" % k, align_bytes=64) for k in range(CHUNKS)]
         out_s = keep.tile([P, T], U8, name="out_s", align_bytes=64)
         out_words = words_of(out_1)
+
+        def slot(k, t):
+            return rounded[k][:].rearrange("p (c t) -> p c t", t=PACK)[:, :, t]
 
         def merge_views(k):
             return (
@@ -243,13 +231,32 @@ def tile_list_rgg_noneP_kernel(
                 pairs[k][:].bitcast(F32).rearrange("p (u c) -> p c u", u=2),
             )
 
-        for k in (0, 1):
-            nc.vector.tensor_copy(out=pair_view(k, 1)[:, :, 1], in_=page_cols(3, k))
-        for k in (0, 1):
-            nc.vector.tensor_copy(*merge_views(k))
+        for h in range(2):
+            for t in range(2):
+                scatter_half(t, h)
+        for t in range(2):
+            nc.sync.dma_start(out=out_rows[t], in_=page[t][:])
+            for k in range(CHUNKS):
+                nc.scalar.copy(out=pair_view(k, 0)[:, :, t], in_=page_cols(t, k))
         for k in (2, 3):
-            nc.scalar.copy(out=pair_view(k, 1)[:, :, 1], in_=page_cols(3, k))
-            nc.scalar.copy(*merge_views(k))
+            to, source = merge_views(k)
+            nc.scalar.copy(out=to[:, :, 0], in_=source[:, :, 0])
+        nc.vector.tensor_tensor(page[2][:].indirect(dst_list[:]), gate[2][:], msg[2][:], MULT)
+        nc.sync.dma_start(out=out_rows[2], in_=page[2][:])
+        for k in (2, 3):
+            nc.scalar.copy(out=slot(k, 2), in_=page_cols(2, k))
+        for k in (0, 1):
+            nc.scalar.copy(out=pair_view(k, 1), in_=page_cols(2, k).unsqueeze(2).to_broadcast([P, CHUNK, 2]))
+            if k == 0:
+                nc.scalar.copy(*merge_views(0))
+        nc.vector.tensor_tensor(page[3][:].indirect(dst_list[:]), gate[3][:], msg[3][:], MULT)
+        nc.sync.dma_start(out=out_rows[3], in_=page[3][:])
+
+        nc.vector.tensor_copy(out=slot(0, 3), in_=page_cols(3, 0))
+        nc.vector.tensor_copy(out=pair_view(1, 1)[:, :, 1], in_=page_cols(3, 1))
+        nc.vector.tensor_copy(*merge_views(1))
+        for k in (2, 3):
+            nc.scalar.copy(out=slot(k, 3), in_=page_cols(3, k))
         for k in range(CHUNKS):
             cols = slice(k * CHUNK, (k + 1) * CHUNK)
             nc.vector.quantize_mx(out=codes[k][:].bitcast(FP8X4), scales=out_s[:, cols], in_=rounded[k][:])

@@ -19,10 +19,18 @@ MULT = mybir.AluOpType.mult
 P = 128
 PACK = 4
 HALF = J // 2
+BLOCKS = HALF // P
 LIST_COLS = J // 16
 BANK = 2048
 CHUNK = 512
 CHUNKS = T // CHUNK
+KB = 1024
+
+AT_FIRST_LOADS = 0
+AT_LATER_LOADS = 12 * KB
+AT_WA_ROUNDED = 24 * KB
+AT_WB_SCALES = 28 * KB
+AT_TURNED = 37 * KB
 
 
 def load_scale_rows(queue, plane, rows):
@@ -43,121 +51,125 @@ def tile_list_rgg_noneP_kernel(
         placed = ctx.enter_context(tc.tile_pool(name="placed", bufs=1))
         psum = ctx.enter_context(tc.psum_pool(name="psum", bufs=1))
 
+        def own(name, shape, dtype):
+            return keep.tile(shape, dtype, name=name, align_bytes=64)
+
+        def at(offset, name, shape, dtype):
+            return placed.tile(shape, dtype, name=name, offset=offset, align_bytes=64)
+
         src_list = keep.tile([P, LIST_COLS], U16, name="src_list")
         dst_list = keep.tile([P, LIST_COLS], U16, name="dst_list")
-        tab_s = keep.tile([P, T], U8, name="tab_s", align_bytes=64)
-        zeros_a = placed.tile([P, P], F32, name="zeros_a", offset=53760, align_bytes=64)
-        zeros = placed.tile([P, 8512], I32, name="zeros", offset=8192, align_bytes=64)
-        wc_s = keep.tile([P, N], U8, name="wc_s", align_bytes=64)
-        ident = keep.tile([P, P], F32, name="ident")
-        wgo_rows = keep.tile([P, P], F32, name="wgo_rows")
-
+        tab_s = own("tab_s", [P, T], U8)
+        wc_s = own("wc_s", [P, N], U8)
+        wb_s = at(AT_WB_SCALES, "wb_s", [P, N], U8)
+        ident = own("ident", [P, P], F32)
+        wgo_rows = own("wgo_rows", [P, P], F32)
+        zeros_table = at(AT_FIRST_LOADS, "zeros_table", [P, 3 * KB], F32)
+        zeros_weights = at(AT_LATER_LOADS, "zeros_weights", [P, 3 * KB], I32)
         warm_in = keep.tile([P, 1], F32, name="warm_in")
         warm = keep.tile([P, 1], F32, name="warm")
+
         nc.vector.memset(tab_s[:].bitcast(I32), 0)
-        nc.vector.memset(zeros_a[:, 0:P], 0.0)
-        nc.vector.memset(zeros[:, 0:P], 0)
+        nc.vector.memset(zeros_table[:, 0:P], 0.0)
+        nc.vector.memset(zeros_weights[:, 0:P], 0)
         nc.vector.memset(warm_in[:], 0.0)
         nc.scalar.activation(out=warm[:], in_=warm_in[:], func=ACT.Sigmoid)
-        nc.vector.tensor_copy(out=wgo_rows[:], in_=zeros_a[:, 0:P])
-        nc.vector.tensor_copy(out=wc_s[:].bitcast(I32), in_=zeros[:, 0:P])
+        nc.vector.tensor_copy(out=wgo_rows[:], in_=zeros_table[:, 0:P])
+        nc.vector.tensor_copy(out=wc_s[:].bitcast(I32), in_=zeros_weights[:, 0:P])
         make_identity(nc, ident[:])
-        wb_s_room = placed.tile([P, 2 * N], U8, name="wb_s_room", offset=14592, align_bytes=64)
-        wb_s = wb_s_room[:, 0:N]
-        nc.gpsimd.memset(wb_s.bitcast(I32), 0)
-        page = [placed.tile([P, T], F32, name="page0", offset=17408, align_bytes=64)]
+        page = [own("page%d" % t, [P, T], F32) for t in range(2)]
         nc.gpsimd.memset(page[0][:], 0.0)
+        nc.gpsimd.memset(wb_s[:].bitcast(I32), 0)
+        nc.gpsimd.memset(page[1][:], 0.0)
 
+        tab_w = at(AT_FIRST_LOADS + 4 * KB, "tab_w", [P, T], I32)
+        wc_w = at(AT_LATER_LOADS, "wc_w", [P, N], I32)
+        wb_w = at(AT_LATER_LOADS + 10 * KB, "wb_w", [P, N], I32)
         wa_raw = [
-            placed.tile([P, PACK, N // 2], F32, name="wa_raw%d" % c, offset=37376 + 4096 * c, align_bytes=64) for c in range(2)
+            at(AT_FIRST_LOADS, "wa_raw0", [P, PACK, N // 2], F32)[:],
+            at(AT_LATER_LOADS + 2 * KB, "wa_raw1", [P, 2 * PACK, N // 2], F32)[:, 0:PACK, :],
         ]
-        wc_w = placed.tile([P, N], I32, name="wc_w", offset=8192, align_bytes=64)
-        wb_w = placed.tile([P, N], I32, name="wb_w", offset=10752, align_bytes=64)
-        tab_w = placed.tile([P, T], I32, name="tab_w", offset=53760, align_bytes=64)
         nc.sync.dma_start(out=src_list[:], in_=offs)
         nc.sync.dma_start(out=dst_list[:], in_=offs2)
         load_scale_rows(nc.sync, tab_s, tab_scales[0])
-        nc.sync.dma_start(out=wgo_rows[0 : J // P, :], in_=wgo[0:1, :].rearrange("o (c p) -> (o c) p", p=P))
-        nc.sync.dma_start(out=tab_w[:], in_=words_of(tab_words))
-        load_scale_rows(nc.sync, wc_s, wc_scales[0])
         wa_rows = wa.rearrange("(p j) n -> p j n", j=PACK)
-        for c in range(2):
-            nc.sync.dma_start(out=wa_raw[c][:], in_=wa_rows[:, :, c * N // 2 : (c + 1) * N // 2])
+        nc.sync.dma_start(out=wa_raw[0], in_=wa_rows[:, :, 0 : N // 2])
+        nc.sync.dma_start(out=tab_w[:], in_=words_of(tab_words))
+        nc.sync.dma_start(out=wgo_rows[0 : J // P, :], in_=wgo[0:1, :].rearrange("o (c p) -> (o c) p", p=P))
+        load_scale_rows(nc.sync, wc_s, wc_scales[0])
         nc.sync.dma_start(out=wc_w[:], in_=words_of(wc_words))
+        nc.sync.dma_start(out=wa_raw[1], in_=wa_rows[:, :, N // 2 : N])
         nc.sync.dma_start(out=wb_w[:], in_=words_of(wb_words))
         load_scale_rows(nc.sync, wb_s, wb_scales[0])
 
-        wa_w = keep.tile([P, N], U32, name="wa_w", align_bytes=64)
-        wa_s = keep.tile([P, N], U8, name="wa_s", align_bytes=64)
-        wa_bf = keep.tile([P, N * PACK], BF16, name="wa_bf", align_bytes=64)
-        for c in range(2):
-            nc.scalar.copy(
-                out=wa_bf[:].rearrange("p (t m j) -> p m t j", t=PACK, j=PACK)[:, c * P // 2 : (c + 1) * P // 2, :, :],
-                in_=wa_raw[c][:].rearrange("p j (m t) -> p m t j", t=PACK),
-            )
+        made = []
 
-        wgo_bank = psum.tile([P, HALF], F32, name="wgo_bank", offset=7 * BANK)
+        def bank(index, span=1):
+            acc = psum.tile([P, span, HALF], F32, name="acc%d" % len(made), offset=index * BANK)
+            made.append(acc)
+            return acc[:, 0, :]
+
+        wgo_bank = bank(7)
         nc.tensor.transpose(wgo_bank[:, 0:P], wgo_rows[:], ident[:])
         wgo_col = keep.tile([P, J // P], F32, name="wgo_col")
         nc.scalar.copy(out=wgo_col[:], in_=wgo_bank[:, 0 : J // P])
 
-        src_s = keep.tile([P, J], U8, name="src_s", align_bytes=64)
-        dst_s = [
-            keep.tile([P, HALF], U8, name="dst_s0", align_bytes=64),
-            placed.tile([P, HALF], U8, name="dst_s1", offset=14848, align_bytes=64),
-        ]
-        src_w = [
-            keep.tile([P, HALF], U32, name="src_w0", align_bytes=64),
-            placed.tile([P, HALF], U32, name="src_w1", offset=12800, align_bytes=64),
-        ]
-        dst_w = [
-            keep.tile([P, HALF], U32, name="dst_w0", align_bytes=64),
-            placed.tile([P, HALF], U32, name="dst_w1", offset=15360, align_bytes=64),
-        ]
+        wbd_w = [own("wbd_w%d" % g, [P, 2 * P], I32) for g in range(2)]
+        wbd_s = [own("wbd_s%d" % g, [P, 2 * P], U8) for g in range(2)]
+        for dealt, loaded in ((wbd_w, wb_w), (wbd_s, wb_s)):
+            for g in range(2):
+                nc.gpsimd.tensor_copy(
+                    out=dealt[g][:].rearrange("p (t m) -> p t m", t=2),
+                    in_=loaded[:].rearrange("p (m t) -> p t m", t=PACK)[:, 2 * g : 2 * g + 2, :],
+                )
+
+        wa_bf = at(AT_WA_ROUNDED, "wa_bf", [P, N * PACK], BF16)
+        wa_w = own("wa_w", [P, N], U32)
+        wa_s = own("wa_s", [P, N], U8)
+        for c in range(2):
+            nc.scalar.copy(
+                out=wa_bf[:].rearrange("p (t m j) -> p m t j", t=PACK, j=PACK)[:, c * P // 2 : (c + 1) * P // 2, :, :],
+                in_=wa_raw[c].rearrange("p j (m t) -> p m t j", t=PACK),
+            )
+
         half_cols = [slice(h * LIST_COLS // 2, (h + 1) * LIST_COLS // 2) for h in range(2)]
         tab_u = tab_w[:].bitcast(U32)
+        src_s = [own("src_s0", [P, HALF], U8)]
+        src_w = [own("src_w0", [P, HALF], U32)]
+        dst_s = [own("dst_s%d" % h, [P, HALF], U8) for h in range(2)]
+        dst_w = [own("dst_w%d" % h, [P, HALF], U32) for h in range(2)]
 
-        nc.vector.tensor_copy(src_s[:], tab_s[:].indirect(src_list[:]))
-        nc.vector.tensor_copy(dst_s[0][:], tab_s[:].indirect(dst_list[:, half_cols[0]]))
-        nc.vector.tensor_copy(src_w[0][:], tab_u.indirect(src_list[:, half_cols[0]]))
-        nc.vector.tensor_copy(dst_w[0][:], tab_u.indirect(dst_list[:, half_cols[0]]))
+        def gather(to, window, offsets, h):
+            nc.vector.tensor_copy(to[h][:], window.indirect(offsets[:, half_cols[h]]))
 
+        gather(src_s, tab_s[:], src_list, 0)
+        gather(dst_s, tab_s[:], dst_list, 0)
+        gather(dst_s, tab_s[:], dst_list, 1)
+        gather(src_w, tab_u, src_list, 0)
+        gather(dst_w, tab_u, dst_list, 0)
+        gather(dst_w, tab_u, dst_list, 1)
         nc.vector.quantize_mx(out=wa_w[:].bitcast(FP8X4), scales=wa_s[:], in_=wa_bf[:])
-        wbd_w = keep.tile([P, N], I32, name="wbd_w", align_bytes=64)
-        wbd_s = keep.tile([P, N], U8, name="wbd_s", align_bytes=64)
-        nc.vector.tensor_copy(out=wbd_w[:].rearrange("p (t m) -> p t m", t=PACK), in_=wb_w[:].rearrange("p (m t) -> p t m", t=PACK))
-        nc.vector.tensor_copy(
-            out=wbd_s[:].rearrange("p (t m) -> p t m", t=PACK),
-            in_=wb_s.rearrange("p (m t) -> p t m", t=PACK),
-        )
-
-        nc.vector.tensor_copy(src_w[1][:], tab_u.indirect(src_list[:, half_cols[1]]))
-        nc.vector.tensor_copy(dst_s[1][:], tab_s[:].indirect(dst_list[:, half_cols[1]]))
-        nc.vector.tensor_copy(dst_w[1][:], tab_u.indirect(dst_list[:, half_cols[1]]))
-
-        page.append(placed.tile([P, T], F32, name="page1", offset=49664, align_bytes=64))
-        page.append(placed.tile([P, T], F32, name="page2", offset=57856, align_bytes=64))
-        nc.gpsimd.memset(page[1][:], 0.0)
+        src_s.append(at(AT_WB_SCALES - HALF // 2, "src_s1", [P, HALF], U8))
+        src_w.append(at(AT_WA_ROUNDED - KB, "src_w1", [P, HALF], U32))
+        gather(src_w, tab_u, src_list, 1)
+        gather(src_s, tab_s[:], src_list, 1)
+        page.append(at(AT_WB_SCALES + HALF // 2, "page2", [P, T], F32))
         nc.gpsimd.memset(page[2][:], 0.0)
+        page.append(page[0])
 
-        msg = [keep.tile([P, J], F32, name="msg%d" % t) for t in range(PACK)]
-        gate = [keep.tile([P, J], F32, name="gate%d" % t) for t in range(PACK)]
-        turned = [keep.tile([P, PACK, P], F32, name="turned%d" % b, align_bytes=64) for b in range(J // P)]
-        made = []
+        msg = [own("msg%d" % t, [P, J], F32) for t in range(PACK)]
+        gate = [own("gate%d" % t, [P, J], F32) for t in range(PACK)]
+        turned = [at(AT_LATER_LOADS + 2 * KB * (1 + b), "turned%d" % b, [P, PACK, P], F32) for b in range(BLOCKS)]
+        turned.extend(at(AT_TURNED + 4 * KB * i, "turned%d" % (BLOCKS + i), [P, PACK, P], F32) for i in range(BLOCKS))
 
-        def banks(first, count):
-            acc = psum.tile([P, count, HALF], F32, name="acc%d" % len(made), offset=first * BANK)
-            made.append(acc)
-            return [acc[:, i, :] for i in range(count)]
-
-        def weighted_messages(h, accs):
-            for i in range(HALF // P):
-                b = h * (HALF // P) + i
-                acc = accs[i]
+        def weighted_messages(h, banks):
+            for i in range(BLOCKS):
+                b = h * BLOCKS + i
+                acc = bank(banks[i])
                 nc.tensor.matmul_mx(
                     out=acc,
                     lhsT=src_w[h][:, i * P : (i + 1) * P].bitcast(FP8X4),
-                    lhsT_scale=src_s[:, b * P : (b + 1) * P],
+                    lhsT_scale=src_s[h][:, i * P : (i + 1) * P],
                     rhs=wc_w[:].bitcast(FP8X4),
                     rhs_scale=wc_s[:],
                     start=True,
@@ -170,57 +182,52 @@ def tile_list_rgg_noneP_kernel(
                     scale=wgo_col[:, b : b + 1],
                 )
 
-        def slice_operands(t, h, back, za):
-            cols = slice(h * HALF, (h + 1) * HALF)
-            rows = slice(t * P, (t + 1) * P)
-            for i in range(HALF // P):
-                nc.tensor.transpose(back[:, i * P : (i + 1) * P], turned[h * (HALF // P) + i][:, t, :], ident[:])
-            nc.tensor.matmul_mx(
-                out=za,
-                lhsT=wbd_w[:, rows].bitcast(FP8X4),
-                lhsT_scale=wbd_s[:, rows],
-                rhs=src_w[h][:].bitcast(FP8X4),
-                rhs_scale=src_s[:, cols],
-                start=True,
-                stop=False,
-            )
-            nc.tensor.matmul_mx(
-                out=za,
-                lhsT=wa_w[:, rows].bitcast(FP8X4),
-                lhsT_scale=wa_s[:, rows],
-                rhs=dst_w[h][:].bitcast(FP8X4),
-                rhs_scale=dst_s[h][:],
-                start=False,
-                stop=True,
-            )
-            nc.scalar.activation(out=gate[t][:, cols], in_=za, func=ACT.Sigmoid)
-            nc.scalar.copy(out=msg[t][:, cols], in_=back)
+        def message_rows(t, h, index):
+            back = bank(index)
+            for i in range(BLOCKS):
+                nc.tensor.transpose(back[:, i * P : (i + 1) * P], turned[h * BLOCKS + i][:, t, :], ident[:])
+            nc.scalar.copy(out=msg[t][:, h * HALF : (h + 1) * HALF], in_=back)
 
-        def scatter_half(t, h):
-            cols = slice(h * HALF, (h + 1) * HALF)
-            nc.vector.tensor_tensor(page[t][:].indirect(dst_list[:, half_cols[h]]), gate[t][:, cols], msg[t][:, cols], MULT)
+        def gate_rows(t, h, za):
+            wb_cols, wa_cols = slice(t % 2 * P, (t % 2 + 1) * P), slice(t * P, (t + 1) * P)
+            passes = [
+                (wbd_w[t // 2][:, wb_cols], wbd_s[t // 2][:, wb_cols], src_w[h], src_s[h]),
+                (wa_w[:, wa_cols], wa_s[:, wa_cols], dst_w[h], dst_s[h]),
+            ]
+            for n, (w_words, w_scales, v_words, v_scales) in enumerate(passes):
+                nc.tensor.matmul_mx(
+                    out=za,
+                    lhsT=w_words.bitcast(FP8X4),
+                    lhsT_scale=w_scales,
+                    rhs=v_words[:].bitcast(FP8X4),
+                    rhs_scale=v_scales[:],
+                    start=n == 0,
+                    stop=n == 1,
+                )
+            nc.scalar.activation(out=gate[t][:, h * HALF : (h + 1) * HALF], in_=za, func=ACT.Sigmoid)
 
-        weighted_messages(0, [banks(i, 1)[0] for i in range(4)])
-        slice_operands(0, 0, banks(4, 4)[0], banks(2, 1)[0])
-        slice_operands(1, 0, banks(3, 1)[0], banks(2, 1)[0])
-        weighted_messages(1, [banks(4 + i, 1)[0] for i in range(4)])
-        for t, h, back, za in ((0, 1, 0, 2), (1, 1, 1, 3), (2, 0, 4, 5), (2, 1, 6, 7), (3, 0, 0, 2), (3, 1, 1, 3)):
-            slice_operands(t, h, banks(back, 1)[0], banks(za, 1)[0])
-        page.append(page[0])
+        weighted_messages(0, (0, 1, 2, 3))
+        gate_rows(0, 0, bank(4, span=3))
+        message_rows(0, 0, 7)
+        message_rows(1, 0, 5)
+        gate_rows(1, 0, bank(6))
+        weighted_messages(1, (0, 1, 2, 3))
+        for t, h, back, za in ((0, 1, 7, 4), (1, 1, 5, 6), (2, 0, 0, 1), (2, 1, 2, 3), (3, 0, 7, 4), (3, 1, 5, 6)):
+            message_rows(t, h, back)
+            gate_rows(t, h, bank(za))
 
         out_rows = out_0.rearrange("(p t) c -> t p c", t=PACK)
-        pairs = [keep.tile([P, 2 * CHUNK * 2], BF16, name="pairs%d" % k, align_bytes=64) for k in range(CHUNKS)]
+        out_words = words_of(out_1)
+        pairs = [at(AT_TURNED + 4 * KB * k, "pairs%d" % k, [P, 2 * CHUNK * 2], BF16) for k in range(CHUNKS)]
+        rounded = [own("rounded%d" % k, [P, CHUNK * PACK], BF16) for k in range(CHUNKS)]
+        codes = [own("codes%d" % k, [P, CHUNK], U32) for k in range(CHUNKS)]
+        out_s = own("out_s", [P, T], U8)
 
         def pair_view(k, u):
             return pairs[k][:].rearrange("p (u c e) -> p u c e", u=2, e=2)[:, u, :, :]
 
         def page_cols(t, k):
             return page[t][:, k * CHUNK : (k + 1) * CHUNK]
-
-        rounded = [keep.tile([P, CHUNK * PACK], BF16, name="rounded%d" % k, align_bytes=64) for k in range(CHUNKS)]
-        codes = [keep.tile([P, CHUNK], U32, name="codes%d" % k, align_bytes=64) for k in range(CHUNKS)]
-        out_s = keep.tile([P, T], U8, name="out_s", align_bytes=64)
-        out_words = words_of(out_1)
 
         def slot(k, t):
             return rounded[k][:].rearrange("p (c t) -> p c t", t=PACK)[:, :, t]
@@ -231,36 +238,40 @@ def tile_list_rgg_noneP_kernel(
                 pairs[k][:].bitcast(F32).rearrange("p (u c) -> p c u", u=2),
             )
 
+        def quantise_out(k):
+            cols = slice(k * CHUNK, (k + 1) * CHUNK)
+            nc.vector.quantize_mx(out=codes[k][:].bitcast(FP8X4), scales=out_s[:, cols], in_=rounded[k][:])
+            nc.sync.dma_start(out=out_words[:, cols], in_=codes[k][:].bitcast(I32))
+
         for h in range(2):
+            cols = slice(h * HALF, (h + 1) * HALF)
             for t in range(2):
-                scatter_half(t, h)
+                nc.vector.tensor_tensor(page[t][:].indirect(dst_list[:, half_cols[h]]), gate[t][:, cols], msg[t][:, cols], MULT)
         for t in range(2):
             nc.sync.dma_start(out=out_rows[t], in_=page[t][:])
             for k in range(CHUNKS):
                 nc.scalar.copy(out=pair_view(k, 0)[:, :, t], in_=page_cols(t, k))
-        for k in (2, 3):
-            to, source = merge_views(k)
-            nc.scalar.copy(out=to[:, :, 0], in_=source[:, :, 0])
+        to, source = merge_views(3)
+        nc.scalar.copy(out=to[:, :, 0], in_=source[:, :, 0])
         nc.vector.tensor_tensor(page[2][:].indirect(dst_list[:]), gate[2][:], msg[2][:], MULT)
         nc.sync.dma_start(out=out_rows[2], in_=page[2][:])
-        for k in (2, 3):
-            nc.scalar.copy(out=slot(k, 2), in_=page_cols(2, k))
-        for k in (0, 1):
-            nc.scalar.copy(out=pair_view(k, 1), in_=page_cols(2, k).unsqueeze(2).to_broadcast([P, CHUNK, 2]))
-            if k == 0:
-                nc.scalar.copy(*merge_views(0))
+        nc.scalar.copy(out=pair_view(0, 1), in_=page_cols(2, 0).unsqueeze(2).to_broadcast([P, CHUNK, 2]))
+        nc.scalar.copy(*merge_views(0))
+        for k in (1, 2):
+            nc.scalar.copy(out=pair_view(k, 1)[:, :, 0], in_=page_cols(2, k))
+        nc.scalar.copy(out=slot(3, 2), in_=page_cols(2, 3))
         nc.vector.tensor_tensor(page[3][:].indirect(dst_list[:]), gate[3][:], msg[3][:], MULT)
         nc.sync.dma_start(out=out_rows[3], in_=page[3][:])
 
+        for k in (1, 2):
+            nc.scalar.copy(out=pair_view(k, 1)[:, :, 1], in_=page_cols(3, k))
+        nc.scalar.copy(out=slot(3, 3), in_=page_cols(3, 3))
         nc.vector.tensor_copy(out=slot(0, 3), in_=page_cols(3, 0))
-        nc.vector.tensor_copy(out=pair_view(1, 1)[:, :, 1], in_=page_cols(3, 1))
         nc.vector.tensor_copy(*merge_views(1))
-        for k in (2, 3):
-            nc.scalar.copy(out=slot(k, 3), in_=page_cols(3, k))
-        for k in range(CHUNKS):
-            cols = slice(k * CHUNK, (k + 1) * CHUNK)
-            nc.vector.quantize_mx(out=codes[k][:].bitcast(FP8X4), scales=out_s[:, cols], in_=rounded[k][:])
-            nc.sync.dma_start(out=out_words[:, cols], in_=codes[k][:].bitcast(I32))
+        quantise_out(0)
+        nc.vector.tensor_copy(*merge_views(2))
+        for k in range(1, CHUNKS):
+            quantise_out(k)
         for q in range(4):
             queue = nc.sync if q % 2 == 0 else nc.scalar
             queue.dma_start(out=out_2[0][4 * q : 4 * q + 4, :].bitcast(I32), in_=out_s[32 * q : 32 * q + 4, :].bitcast(I32))

@@ -27,10 +27,11 @@ CHUNKS = T // CHUNK
 KB = 1024
 
 AT_FIRST_LOADS = 0
-AT_LATER_LOADS = 12 * KB
-AT_WA_ROUNDED = 24 * KB
-AT_WB_SCALES = 28 * KB
-AT_TURNED = 37 * KB
+AT_PAGES = 2 * KB
+AT_LATER_LOADS = 18 * KB
+AT_WA_ROUNDED = 28 * KB
+AT_WB_SCALES = 32 * KB
+AT_TURNED = 35 * KB
 
 
 def load_scale_rows(queue, plane, rows):
@@ -64,8 +65,8 @@ def tile_list_rgg_noneP_kernel(
         wb_s = at(AT_WB_SCALES, "wb_s", [P, N], U8)
         ident = own("ident", [P, P], F32)
         wgo_rows = own("wgo_rows", [P, P], F32)
-        zeros_table = at(AT_FIRST_LOADS, "zeros_table", [P, 3 * KB], F32)
-        zeros_weights = at(AT_LATER_LOADS, "zeros_weights", [P, 3 * KB], I32)
+        zeros_table = at(AT_FIRST_LOADS, "zeros_table", [P, 14 * KB // 4], F32)
+        zeros_weights = at(AT_LATER_LOADS, "zeros_weights", [P, 10 * KB // 4], I32)
         warm_in = keep.tile([P, 1], F32, name="warm_in")
         warm = keep.tile([P, 1], F32, name="warm")
 
@@ -77,29 +78,28 @@ def tile_list_rgg_noneP_kernel(
         nc.vector.tensor_copy(out=wgo_rows[:], in_=zeros_table[:, 0:P])
         nc.vector.tensor_copy(out=wc_s[:].bitcast(I32), in_=zeros_weights[:, 0:P])
         make_identity(nc, ident[:])
-        page = [own("page%d" % t, [P, T], F32) for t in range(2)]
-        nc.gpsimd.memset(page[0][:], 0.0)
-        nc.gpsimd.memset(wb_s[:].bitcast(I32), 0)
-        nc.gpsimd.memset(page[1][:], 0.0)
+        nc.vector.memset(wb_s[:].bitcast(I32), 0)
+        page = [own("page0", [P, T], F32)]
+        nc.vector.memset(page[0][:], 0.0)
 
-        tab_w = at(AT_FIRST_LOADS + 4 * KB, "tab_w", [P, T], I32)
+        tab_w = at(AT_FIRST_LOADS + 6 * KB, "tab_w", [P, T], I32)
         wc_w = at(AT_LATER_LOADS, "wc_w", [P, N], I32)
-        wb_w = at(AT_LATER_LOADS + 10 * KB, "wb_w", [P, N], I32)
+        wb_w = at(AT_FIRST_LOADS, "wb_w", [P, N], I32)
         wa_raw = [
-            at(AT_FIRST_LOADS, "wa_raw0", [P, PACK, N // 2], F32)[:],
+            at(AT_FIRST_LOADS + 2 * KB, "wa_raw0", [P, PACK, N // 2], F32)[:],
             at(AT_LATER_LOADS + 2 * KB, "wa_raw1", [P, 2 * PACK, N // 2], F32)[:, 0:PACK, :],
         ]
         nc.sync.dma_start(out=src_list[:], in_=offs)
         nc.sync.dma_start(out=dst_list[:], in_=offs2)
         load_scale_rows(nc.sync, tab_s, tab_scales[0])
         wa_rows = wa.rearrange("(p j) n -> p j n", j=PACK)
+        nc.sync.dma_start(out=wb_w[:], in_=words_of(wb_words))
         nc.sync.dma_start(out=wa_raw[0], in_=wa_rows[:, :, 0 : N // 2])
         nc.sync.dma_start(out=tab_w[:], in_=words_of(tab_words))
         nc.sync.dma_start(out=wgo_rows[0 : J // P, :], in_=wgo[0:1, :].rearrange("o (c p) -> (o c) p", p=P))
         load_scale_rows(nc.sync, wc_s, wc_scales[0])
-        nc.sync.dma_start(out=wc_w[:], in_=words_of(wc_words))
         nc.sync.dma_start(out=wa_raw[1], in_=wa_rows[:, :, N // 2 : N])
-        nc.sync.dma_start(out=wb_w[:], in_=words_of(wb_words))
+        nc.sync.dma_start(out=wc_w[:], in_=words_of(wc_words))
         load_scale_rows(nc.sync, wb_s, wb_scales[0])
 
         made = []
@@ -114,14 +114,12 @@ def tile_list_rgg_noneP_kernel(
         wgo_col = keep.tile([P, J // P], F32, name="wgo_col")
         nc.scalar.copy(out=wgo_col[:], in_=wgo_bank[:, 0 : J // P])
 
-        wbd_w = [own("wbd_w%d" % g, [P, 2 * P], I32) for g in range(2)]
-        wbd_s = [own("wbd_s%d" % g, [P, 2 * P], U8) for g in range(2)]
-        for dealt, loaded in ((wbd_w, wb_w), (wbd_s, wb_s)):
-            for g in range(2):
-                nc.gpsimd.tensor_copy(
-                    out=dealt[g][:].rearrange("p (t m) -> p t m", t=2),
-                    in_=loaded[:].rearrange("p (m t) -> p t m", t=PACK)[:, 2 * g : 2 * g + 2, :],
-                )
+        wbd_w = own("wbd_w", [P, N], U32)
+        wbd_s = own("wbd_s", [P, N], U8)
+        nc.scalar.copy(
+            out=wbd_w[:].rearrange("p (t m) -> p t m", t=PACK),
+            in_=wb_w[:].bitcast(U32).rearrange("p (m t) -> p t m", t=PACK),
+        )
 
         wa_bf = at(AT_WA_ROUNDED, "wa_bf", [P, N * PACK], BF16)
         wa_w = own("wa_w", [P, N], U32)
@@ -134,27 +132,31 @@ def tile_list_rgg_noneP_kernel(
 
         half_cols = [slice(h * LIST_COLS // 2, (h + 1) * LIST_COLS // 2) for h in range(2)]
         tab_u = tab_w[:].bitcast(U32)
-        src_s = [own("src_s0", [P, HALF], U8)]
-        src_w = [own("src_w0", [P, HALF], U32)]
+        src_s = [own("src_s%d" % h, [P, HALF], U8) for h in range(2)]
         dst_s = [own("dst_s%d" % h, [P, HALF], U8) for h in range(2)]
-        dst_w = [own("dst_w%d" % h, [P, HALF], U32) for h in range(2)]
+        src_w = [own("src_w0", [P, HALF], U32)]
+        dst_w = [own("dst_w0", [P, HALF], U32)]
 
         def gather(to, window, offsets, h):
             nc.vector.tensor_copy(to[h][:], window.indirect(offsets[:, half_cols[h]]))
 
-        gather(src_s, tab_s[:], src_list, 0)
-        gather(dst_s, tab_s[:], dst_list, 0)
-        gather(dst_s, tab_s[:], dst_list, 1)
+        for h in range(2):
+            gather(src_s, tab_s[:], src_list, h)
+            gather(dst_s, tab_s[:], dst_list, h)
         gather(src_w, tab_u, src_list, 0)
         gather(dst_w, tab_u, dst_list, 0)
-        gather(dst_w, tab_u, dst_list, 1)
         nc.vector.quantize_mx(out=wa_w[:].bitcast(FP8X4), scales=wa_s[:], in_=wa_bf[:])
-        src_s.append(at(AT_WB_SCALES - HALF // 2, "src_s1", [P, HALF], U8))
-        src_w.append(at(AT_WA_ROUNDED - KB, "src_w1", [P, HALF], U32))
+        nc.vector.tensor_copy(
+            out=wbd_s[:].rearrange("p (t m) -> p t m", t=PACK),
+            in_=wb_s[:].rearrange("p (m t) -> p t m", t=PACK),
+        )
+        dst_w.append(at(AT_WB_SCALES + N // 2 - 2 * KB, "dst_w1", [P, HALF], U32))
+        src_w.append(at(AT_WB_SCALES + N // 2, "src_w1", [P, HALF], U32))
+        gather(dst_w, tab_u, dst_list, 1)
         gather(src_w, tab_u, src_list, 1)
-        gather(src_s, tab_s[:], src_list, 1)
-        page.append(at(AT_WB_SCALES + HALF // 2, "page2", [P, T], F32))
-        nc.gpsimd.memset(page[2][:], 0.0)
+        for t in (1, 2):
+            page.append(at(AT_PAGES + 8 * KB * (t - 1), "page%d" % t, [P, T], F32))
+            nc.gpsimd.memset(page[t][:], 0.0)
         page.append(page[0])
 
         msg = [own("msg%d" % t, [P, J], F32) for t in range(PACK)]
@@ -189,10 +191,10 @@ def tile_list_rgg_noneP_kernel(
             nc.scalar.copy(out=msg[t][:, h * HALF : (h + 1) * HALF], in_=back)
 
         def gate_rows(t, h, za):
-            wb_cols, wa_cols = slice(t % 2 * P, (t % 2 + 1) * P), slice(t * P, (t + 1) * P)
+            rows = slice(t * P, (t + 1) * P)
             passes = [
-                (wbd_w[t // 2][:, wb_cols], wbd_s[t // 2][:, wb_cols], src_w[h], src_s[h]),
-                (wa_w[:, wa_cols], wa_s[:, wa_cols], dst_w[h], dst_s[h]),
+                (wa_w[:, rows], wa_s[:, rows], dst_w[h], dst_s[h]),
+                (wbd_w[:, rows], wbd_s[:, rows], src_w[h], src_s[h]),
             ]
             for n, (w_words, w_scales, v_words, v_scales) in enumerate(passes):
                 nc.tensor.matmul_mx(

@@ -24,6 +24,7 @@ LIST_COLS = J // 16
 BANK = 2048
 CHUNK = 512
 CHUNKS = T // CHUNK
+PIECE = CHUNK // 2
 KB = 1024
 
 AT_FIRST_LOADS = 0
@@ -132,17 +133,18 @@ def tile_list_rgg_noneP_kernel(
 
         half_cols = [slice(h * LIST_COLS // 2, (h + 1) * LIST_COLS // 2) for h in range(2)]
         tab_u = tab_w[:].bitcast(U32)
-        src_s = [own("src_s%d" % h, [P, HALF], U8) for h in range(2)]
-        dst_s = [own("dst_s%d" % h, [P, HALF], U8) for h in range(2)]
+        src_scales = own("src_scales", [P, J], U8)
+        dst_scales = own("dst_scales", [P, J], U8)
+        src_s = [src_scales[:, h * HALF : (h + 1) * HALF] for h in range(2)]
+        dst_s = [dst_scales[:, h * HALF : (h + 1) * HALF] for h in range(2)]
         src_w = [own("src_w0", [P, HALF], U32)]
         dst_w = [own("dst_w0", [P, HALF], U32)]
 
         def gather(to, window, offsets, h):
             nc.vector.tensor_copy(to[h][:], window.indirect(offsets[:, half_cols[h]]))
 
-        for h in range(2):
-            gather(src_s, tab_s[:], src_list, h)
-            gather(dst_s, tab_s[:], dst_list, h)
+        nc.vector.tensor_copy(src_scales[:], tab_s[:].indirect(src_list[:]))
+        nc.vector.tensor_copy(dst_scales[:], tab_s[:].indirect(dst_list[:]))
         gather(src_w, tab_u, src_list, 0)
         gather(dst_w, tab_u, dst_list, 0)
         nc.vector.quantize_mx(out=wa_w[:].bitcast(FP8X4), scales=wa_s[:], in_=wa_bf[:])
@@ -202,7 +204,7 @@ def tile_list_rgg_noneP_kernel(
                     lhsT=w_words.bitcast(FP8X4),
                     lhsT_scale=w_scales,
                     rhs=v_words[:].bitcast(FP8X4),
-                    rhs_scale=v_scales[:],
+                    rhs_scale=v_scales,
                     start=n == 0,
                     stop=n == 1,
                 )
@@ -223,7 +225,13 @@ def tile_list_rgg_noneP_kernel(
         pairs = [at(AT_TURNED + 4 * KB * k, "pairs%d" % k, [P, 2 * CHUNK * 2], BF16) for k in range(CHUNKS)]
         rounded = [own("rounded%d" % k, [P, CHUNK * PACK], BF16) for k in range(CHUNKS)]
         codes = [own("codes%d" % k, [P, CHUNK], U32) for k in range(CHUNKS)]
-        out_s = own("out_s", [P, T], U8)
+        out_s = own("out_s", [P, CHUNK], U8)
+
+        def within(piece):
+            return slice(piece % 2 * PIECE, (piece % 2 + 1) * PIECE)
+
+        def span(first, last):
+            return first // 2, slice(within(first).start, within(last).stop)
 
         def pair_view(k, u):
             return pairs[k][:].rearrange("p (u c e) -> p u c e", u=2, e=2)[:, u, :, :]
@@ -234,17 +242,25 @@ def tile_list_rgg_noneP_kernel(
         def slot(k, t):
             return rounded[k][:].rearrange("p (c t) -> p c t", t=PACK)[:, :, t]
 
-        def merge_views(k):
+        def merge_views(k, cols):
             return (
-                rounded[k][:].bitcast(F32).rearrange("p (c u) -> p c u", u=2),
-                pairs[k][:].bitcast(F32).rearrange("p (u c) -> p c u", u=2),
+                rounded[k][:].bitcast(F32).rearrange("p (c u) -> p c u", u=2)[:, cols, :],
+                pairs[k][:].bitcast(F32).rearrange("p (u c) -> p c u", u=2)[:, cols, :],
             )
 
-        def quantise_out(k):
-            cols = slice(k * CHUNK, (k + 1) * CHUNK)
-            nc.vector.quantize_mx(out=codes[k][:].bitcast(FP8X4), scales=out_s[:, cols], in_=rounded[k][:])
-            nc.sync.dma_start(out=out_words[:, cols], in_=codes[k][:].bitcast(I32))
+        def quantise_out(piece):
+            k, cols = span(piece, piece)
+            nc.vector.quantize_mx(
+                out=codes[k][:, cols].bitcast(FP8X4),
+                scales=out_s[4 * k : P, cols],
+                in_=rounded[k][:, PACK * cols.start : PACK * cols.stop],
+            )
 
+        def store_codes(k, cols):
+            nc.sync.dma_start(out=out_words[:, k * CHUNK : (k + 1) * CHUNK][:, cols], in_=codes[k][:, cols].bitcast(I32))
+
+        merged_late = [span(2, 3), span(4, 4)]
+        placed_early = [span(5, 5), span(6, 7)]
         for h in range(2):
             cols = slice(h * HALF, (h + 1) * HALF)
             for t in range(2):
@@ -253,27 +269,39 @@ def tile_list_rgg_noneP_kernel(
             nc.sync.dma_start(out=out_rows[t], in_=page[t][:])
             for k in range(CHUNKS):
                 nc.scalar.copy(out=pair_view(k, 0)[:, :, t], in_=page_cols(t, k))
-        to, source = merge_views(3)
-        nc.scalar.copy(out=to[:, :, 0], in_=source[:, :, 0])
+        for k, cols in placed_early:
+            to, source = merge_views(k, cols)
+            nc.scalar.copy(out=to[:, :, 0], in_=source[:, :, 0])
         nc.vector.tensor_tensor(page[2][:].indirect(dst_list[:]), gate[2][:], msg[2][:], MULT)
         nc.sync.dma_start(out=out_rows[2], in_=page[2][:])
         nc.scalar.copy(out=pair_view(0, 1), in_=page_cols(2, 0).unsqueeze(2).to_broadcast([P, CHUNK, 2]))
-        nc.scalar.copy(*merge_views(0))
-        for k in (1, 2):
-            nc.scalar.copy(out=pair_view(k, 1)[:, :, 0], in_=page_cols(2, k))
-        nc.scalar.copy(out=slot(3, 2), in_=page_cols(2, 3))
+        nc.scalar.copy(*merge_views(0, slice(0, CHUNK)))
+        for k, cols in merged_late:
+            nc.scalar.copy(out=pair_view(k, 1)[:, cols, 0], in_=page_cols(2, k)[:, cols])
+        for k, cols in placed_early:
+            nc.scalar.copy(out=slot(k, 2)[:, cols], in_=page_cols(2, k)[:, cols])
         nc.vector.tensor_tensor(page[3][:].indirect(dst_list[:]), gate[3][:], msg[3][:], MULT)
         nc.sync.dma_start(out=out_rows[3], in_=page[3][:])
 
-        for k in (1, 2):
-            nc.scalar.copy(out=pair_view(k, 1)[:, :, 1], in_=page_cols(3, k))
-        nc.scalar.copy(out=slot(3, 3), in_=page_cols(3, 3))
-        nc.vector.tensor_copy(out=slot(0, 3), in_=page_cols(3, 0))
-        nc.vector.tensor_copy(*merge_views(1))
+        for k, cols in merged_late:
+            nc.scalar.copy(out=pair_view(k, 1)[:, cols, 1], in_=page_cols(3, k)[:, cols])
+        for piece in (5, 6, 7):
+            k, cols = span(piece, piece)
+            nc.scalar.copy(out=slot(k, 3)[:, cols], in_=page_cols(3, k)[:, cols])
+        for piece in (0, 1):
+            nc.vector.tensor_copy(out=slot(0, 3)[:, within(piece)], in_=page_cols(3, 0)[:, within(piece)])
         quantise_out(0)
-        nc.vector.tensor_copy(*merge_views(2))
-        for k in range(1, CHUNKS):
-            quantise_out(k)
+        for piece in range(1, 2 * CHUNKS):
+            if piece + 1 in (2, 3, 4):
+                nc.vector.tensor_copy(*merge_views(*span(piece + 1, piece + 1)))
+            quantise_out(piece)
+            if piece in (1, 3, 5):
+                store_codes(*span(piece - 1, piece))
+            if piece in (6, 7):
+                store_codes(*span(piece, piece))
         for q in range(4):
             queue = nc.sync if q % 2 == 0 else nc.scalar
-            queue.dma_start(out=out_2[0][4 * q : 4 * q + 4, :].bitcast(I32), in_=out_s[32 * q : 32 * q + 4, :].bitcast(I32))
+            queue.dma_start(
+                out=out_2[0][4 * q : 4 * q + 4, :].bitcast(I32).rearrange("r (k c) -> k r c", k=CHUNKS),
+                in_=out_s[32 * q : 32 * q + 4 * CHUNKS, :].bitcast(I32),
+            )

@@ -66,8 +66,8 @@ def tile_list_rgg_noneP_kernel(
         wb_s = at(AT_WB_SCALES, "wb_s", [P, N], U8)
         ident = own("ident", [P, P], F32)
         wgo_rows = own("wgo_rows", [P, P], F32)
-        zeros_table = at(AT_FIRST_LOADS, "zeros_table", [P, 14 * KB // 4], F32)
-        zeros_weights = at(AT_LATER_LOADS, "zeros_weights", [P, 10 * KB // 4], I32)
+        zeros_table = at(AT_FIRST_LOADS, "zeros_table", [P, 6 * KB // 4], F32)
+        zeros_weights = at(AT_FIRST_LOADS + 6 * KB, "zeros_weights", [P, 22 * KB // 4], I32)
         warm_in = keep.tile([P, 1], F32, name="warm_in")
         warm = keep.tile([P, 1], F32, name="warm")
 
@@ -96,9 +96,9 @@ def tile_list_rgg_noneP_kernel(
         wa_rows = wa.rearrange("(p j) n -> p j n", j=PACK)
         nc.sync.dma_start(out=wb_w[:], in_=words_of(wb_words))
         nc.sync.dma_start(out=wa_raw[0], in_=wa_rows[:, :, 0 : N // 2])
+        load_scale_rows(nc.sync, wc_s, wc_scales[0])
         nc.sync.dma_start(out=tab_w[:], in_=words_of(tab_words))
         nc.sync.dma_start(out=wgo_rows[0 : J // P, :], in_=wgo[0:1, :].rearrange("o (c p) -> (o c) p", p=P))
-        load_scale_rows(nc.sync, wc_s, wc_scales[0])
         nc.sync.dma_start(out=wa_raw[1], in_=wa_rows[:, :, N // 2 : N])
         nc.sync.dma_start(out=wc_w[:], in_=words_of(wc_words))
         load_scale_rows(nc.sync, wb_s, wb_scales[0])
@@ -163,13 +163,12 @@ def tile_list_rgg_noneP_kernel(
 
         msg = [own("msg%d" % t, [P, J], F32) for t in range(PACK)]
         gate = [own("gate%d" % t, [P, J], F32) for t in range(PACK)]
-        turned = [at(AT_LATER_LOADS + 2 * KB * (1 + b), "turned%d" % b, [P, PACK, P], F32) for b in range(BLOCKS)]
-        turned.extend(at(AT_TURNED + 4 * KB * i, "turned%d" % (BLOCKS + i), [P, PACK, P], F32) for i in range(BLOCKS))
+        turned_at = [AT_LATER_LOADS + 2 * KB * (1 + i) for i in range(BLOCKS)] + [AT_TURNED + 4 * KB * i for i in range(BLOCKS)]
+        turned = {}
 
-        def weighted_messages(h, banks):
-            for i in range(BLOCKS):
-                b = h * BLOCKS + i
-                acc = bank(banks[i])
+        def message_passes(h, banks):
+            accs = [bank(i) for i in banks]
+            for i, acc in enumerate(accs):
                 nc.tensor.matmul_mx(
                     out=acc,
                     lhsT=src_w[h][:, i * P : (i + 1) * P].bitcast(FP8X4),
@@ -179,9 +178,15 @@ def tile_list_rgg_noneP_kernel(
                     start=True,
                     stop=True,
                 )
+            return accs
+
+        def weigh_messages(h, accs, g):
+            for i, acc in enumerate(accs):
+                b = h * BLOCKS + i
+                turned[b, g] = at(turned_at[b], "turned%d_%d" % (b, g), [P, 2, P], F32)
                 nc.scalar.activation(
-                    out=turned[b][:],
-                    in_=acc.rearrange("p (m t) -> p t m", t=PACK),
+                    out=turned[b, g][:],
+                    in_=acc.rearrange("p (m t) -> p t m", t=PACK)[:, 2 * g : 2 * g + 2, :],
                     func=ACT.Copy,
                     scale=wgo_col[:, b : b + 1],
                 )
@@ -189,7 +194,7 @@ def tile_list_rgg_noneP_kernel(
         def message_rows(t, h, index):
             back = bank(index)
             for i in range(BLOCKS):
-                nc.tensor.transpose(back[:, i * P : (i + 1) * P], turned[h * BLOCKS + i][:, t, :], ident[:])
+                nc.tensor.transpose(back[:, i * P : (i + 1) * P], turned[h * BLOCKS + i, t // 2][:, t % 2, :], ident[:])
             nc.scalar.copy(out=msg[t][:, h * HALF : (h + 1) * HALF], in_=back)
 
         def gate_rows(t, h, za):
@@ -210,13 +215,20 @@ def tile_list_rgg_noneP_kernel(
                 )
             nc.scalar.activation(out=gate[t][:, h * HALF : (h + 1) * HALF], in_=za, func=ACT.Sigmoid)
 
-        weighted_messages(0, (0, 1, 2, 3))
+        accs = message_passes(0, (0, 1, 2, 3))
+        weigh_messages(0, accs, 0)
         gate_rows(0, 0, bank(4, span=3))
         message_rows(0, 0, 7)
         message_rows(1, 0, 5)
         gate_rows(1, 0, bank(6))
-        weighted_messages(1, (0, 1, 2, 3))
-        for t, h, back, za in ((0, 1, 7, 4), (1, 1, 5, 6), (2, 0, 0, 1), (2, 1, 2, 3), (3, 0, 7, 4), (3, 1, 5, 6)):
+        later_accs = message_passes(1, (7, 4, 5, 6))
+        weigh_messages(1, later_accs, 0)
+        weigh_messages(0, accs, 1)
+        for t, h, back, za in ((0, 1, 0, 1), (1, 1, 2, 3)):
+            message_rows(t, h, back)
+            gate_rows(t, h, bank(za))
+        weigh_messages(1, later_accs, 1)
+        for t, h, back, za in ((2, 0, 7, 4), (2, 1, 5, 6), (3, 0, 0, 1), (3, 1, 2, 3)):
             message_rows(t, h, back)
             gate_rows(t, h, bank(za))
 

@@ -27,17 +27,18 @@ CHUNKS = T // CHUNK
 PIECE = CHUNK // 2
 KB = 1024
 
-AT_FIRST_LOADS = 0
-AT_PAGES = 2 * KB
-AT_LATER_LOADS = 18 * KB
-AT_WA_ROUNDED = 28 * KB
-AT_WB_SCALES = 32 * KB
-AT_TURNED = 35 * KB
+AT_PAGE0 = 0
+AT_FIRST_LOADS = 8 * KB
+AT_PAGES = 10 * KB
+AT_LATER_LOADS = 26 * KB
+AT_WA_ROUNDED = 36 * KB
+AT_WB_SCALES = 40 * KB
+AT_TURNED = 43 * KB
 
 
 def load_scale_rows(queue, plane, rows):
-    for q in range(4):
-        queue.dma_start(out=plane[32 * q : 32 * q + 4, :].bitcast(I32), in_=rows[4 * q : 4 * q + 4, :].bitcast(I32))
+    for r in range(4):
+        queue.dma_start(out=plane[r:P:32, :].bitcast(I32), in_=rows[r:16:4, :].bitcast(I32))
 
 
 def words_of(packed):
@@ -65,27 +66,24 @@ def tile_list_rgg_noneP_kernel(
         wc_s = own("wc_s", [P, N], U8)
         wb_s = at(AT_WB_SCALES, "wb_s", [P, N], U8)
         ident = own("ident", [P, P], F32)
-        wgo_rows = own("wgo_rows", [P, P], F32)
-        zeros_table = at(AT_FIRST_LOADS, "zeros_table", [P, 6 * KB // 4], F32)
-        zeros_weights = at(AT_FIRST_LOADS + 6 * KB, "zeros_weights", [P, 22 * KB // 4], I32)
+        zeros_weights = at(AT_PAGE0, "zeros_weights", [P, AT_WA_ROUNDED // 4], I32)
         warm_in = keep.tile([P, 1], F32, name="warm_in")
         warm = keep.tile([P, 1], F32, name="warm")
 
         nc.vector.memset(tab_s[:].bitcast(I32), 0)
-        nc.vector.memset(zeros_table[:, 0:P], 0.0)
         nc.vector.memset(zeros_weights[:, 0:P], 0)
         nc.vector.memset(warm_in[:], 0.0)
         nc.scalar.activation(out=warm[:], in_=warm_in[:], func=ACT.Sigmoid)
-        nc.vector.tensor_copy(out=wgo_rows[:], in_=zeros_table[:, 0:P])
         nc.vector.tensor_copy(out=wc_s[:].bitcast(I32), in_=zeros_weights[:, 0:P])
         make_identity(nc, ident[:])
         nc.vector.memset(wb_s[:].bitcast(I32), 0)
-        page = [own("page0", [P, T], F32)]
+        page = [at(AT_PAGE0, "page0", [P, T], F32)]
         nc.vector.memset(page[0][:], 0.0)
 
         tab_w = at(AT_FIRST_LOADS + 6 * KB, "tab_w", [P, T], I32)
         wc_w = at(AT_LATER_LOADS, "wc_w", [P, N], I32)
         wb_w = at(AT_FIRST_LOADS, "wb_w", [P, N], I32)
+        wgo_rows = at(AT_FIRST_LOADS + 14 * KB, "wgo_rows", [P, P], F32)
         wa_raw = [
             at(AT_FIRST_LOADS + 2 * KB, "wa_raw0", [P, PACK, N // 2], F32)[:],
             at(AT_LATER_LOADS + 2 * KB, "wa_raw1", [P, 2 * PACK, N // 2], F32)[:, 0:PACK, :],
@@ -98,7 +96,7 @@ def tile_list_rgg_noneP_kernel(
         nc.sync.dma_start(out=wa_raw[0], in_=wa_rows[:, :, 0 : N // 2])
         load_scale_rows(nc.sync, wc_s, wc_scales[0])
         nc.sync.dma_start(out=tab_w[:], in_=words_of(tab_words))
-        nc.sync.dma_start(out=wgo_rows[0 : J // P, :], in_=wgo[0:1, :].rearrange("o (c p) -> (o c) p", p=P))
+        nc.sync.dma_start(out=wgo_rows[:], in_=wgo[0 : P * P // J, :].rearrange("o (c p) -> (o c) p", p=P))
         nc.sync.dma_start(out=wa_raw[1], in_=wa_rows[:, :, N // 2 : N])
         nc.sync.dma_start(out=wc_w[:], in_=words_of(wc_words))
         load_scale_rows(nc.sync, wb_s, wb_scales[0])

@@ -27,7 +27,6 @@ CHUNKS = T // CHUNK
 PIECE = CHUNK // 2
 KB = 1024
 
-AT_PAGE0 = 0
 AT_FIRST_LOADS = 8 * KB
 AT_PAGES = 10 * KB
 AT_LATER_LOADS = 26 * KB
@@ -37,8 +36,8 @@ AT_TURNED = 43 * KB
 
 
 def load_scale_rows(queue, plane, rows):
-    for r in range(4):
-        queue.dma_start(out=plane[r:P:32, :].bitcast(I32), in_=rows[r:16:4, :].bitcast(I32))
+    for q in range(4):
+        queue.dma_start(out=plane[32 * q : 32 * q + 4, :].bitcast(I32), in_=rows[4 * q : 4 * q + 4, :].bitcast(I32))
 
 
 def words_of(packed):
@@ -66,19 +65,19 @@ def tile_list_rgg_noneP_kernel(
         wc_s = own("wc_s", [P, N], U8)
         wb_s = at(AT_WB_SCALES, "wb_s", [P, N], U8)
         ident = own("ident", [P, P], F32)
-        zeros_weights = at(AT_PAGE0, "zeros_weights", [P, AT_WA_ROUNDED // 4], I32)
+        zeros_weights = at(AT_FIRST_LOADS, "zeros_weights", [P, (AT_WA_ROUNDED - AT_FIRST_LOADS) // 4], I32)
         warm_in = keep.tile([P, 1], F32, name="warm_in")
         warm = keep.tile([P, 1], F32, name="warm")
 
+        page = [own("page0", [P, T], F32)]
         nc.vector.memset(tab_s[:].bitcast(I32), 0)
-        nc.vector.memset(zeros_weights[:, 0:P], 0)
         nc.vector.memset(warm_in[:], 0.0)
         nc.scalar.activation(out=warm[:], in_=warm_in[:], func=ACT.Sigmoid)
-        nc.vector.tensor_copy(out=wc_s[:].bitcast(I32), in_=zeros_weights[:, 0:P])
-        make_identity(nc, ident[:])
-        nc.vector.memset(wb_s[:].bitcast(I32), 0)
-        page = [at(AT_PAGE0, "page0", [P, T], F32)]
+        nc.vector.memset(zeros_weights[:, 0:P], 0)
         nc.vector.memset(page[0][:], 0.0)
+        nc.vector.tensor_copy(out=wc_s[:].bitcast(I32), in_=zeros_weights[:, 0:P])
+        nc.vector.memset(wb_s[:].bitcast(I32), 0)
+        make_identity(nc, ident[:])
 
         tab_w = at(AT_FIRST_LOADS + 6 * KB, "tab_w", [P, T], I32)
         wc_w = at(AT_LATER_LOADS, "wc_w", [P, N], I32)
@@ -92,13 +91,13 @@ def tile_list_rgg_noneP_kernel(
         nc.sync.dma_start(out=dst_list[:], in_=offs2)
         load_scale_rows(nc.sync, tab_s, tab_scales[0])
         wa_rows = wa.rearrange("(p j) n -> p j n", j=PACK)
-        nc.sync.dma_start(out=wb_w[:], in_=words_of(wb_words))
         nc.sync.dma_start(out=wa_raw[0], in_=wa_rows[:, :, 0 : N // 2])
-        load_scale_rows(nc.sync, wc_s, wc_scales[0])
         nc.sync.dma_start(out=tab_w[:], in_=words_of(tab_words))
+        load_scale_rows(nc.sync, wc_s, wc_scales[0])
         nc.sync.dma_start(out=wgo_rows[:], in_=wgo[0 : P * P // J, :].rearrange("o (c p) -> (o c) p", p=P))
         nc.sync.dma_start(out=wa_raw[1], in_=wa_rows[:, :, N // 2 : N])
         nc.sync.dma_start(out=wc_w[:], in_=words_of(wc_words))
+        nc.sync.dma_start(out=wb_w[:], in_=words_of(wb_words))
         load_scale_rows(nc.sync, wb_s, wb_scales[0])
 
         made = []
@@ -113,13 +112,6 @@ def tile_list_rgg_noneP_kernel(
         wgo_col = keep.tile([P, J // P], F32, name="wgo_col")
         nc.scalar.copy(out=wgo_col[:], in_=wgo_bank[:, 0 : J // P])
 
-        wbd_w = own("wbd_w", [P, N], U32)
-        wbd_s = own("wbd_s", [P, N], U8)
-        nc.scalar.copy(
-            out=wbd_w[:].rearrange("p (t m) -> p t m", t=PACK),
-            in_=wb_w[:].bitcast(U32).rearrange("p (m t) -> p t m", t=PACK),
-        )
-
         wa_bf = at(AT_WA_ROUNDED, "wa_bf", [P, N * PACK], BF16)
         wa_w = own("wa_w", [P, N], U32)
         wa_s = own("wa_s", [P, N], U8)
@@ -129,6 +121,16 @@ def tile_list_rgg_noneP_kernel(
                 in_=wa_raw[c].rearrange("p j (m t) -> p m t j", t=PACK),
             )
 
+        wbd_w = [own("wbd_w%d" % g, [P, 2 * P], U32) for g in range(2)]
+        wbd_s = own("wbd_s", [P, N], U8)
+
+        def deal_wb_words(g):
+            nc.scalar.copy(
+                out=wbd_w[g][:].rearrange("p (t m) -> p m t", t=2),
+                in_=wb_w[:].bitcast(U32).rearrange("p (m t) -> p m t", t=PACK)[:, :, 2 * g : 2 * g + 2],
+            )
+
+        deal_wb_words(0)
         half_cols = [slice(h * LIST_COLS // 2, (h + 1) * LIST_COLS // 2) for h in range(2)]
         tab_u = tab_w[:].bitcast(U32)
         src_scales = own("src_scales", [P, J], U8)
@@ -199,7 +201,7 @@ def tile_list_rgg_noneP_kernel(
             rows = slice(t * P, (t + 1) * P)
             passes = [
                 (wa_w[:, rows], wa_s[:, rows], dst_w[h], dst_s[h]),
-                (wbd_w[:, rows], wbd_s[:, rows], src_w[h], src_s[h]),
+                (wbd_w[t // 2][:, t % 2 * P : (t % 2 + 1) * P], wbd_s[:, rows], src_w[h], src_s[h]),
             ]
             for n, (w_words, w_scales, v_words, v_scales) in enumerate(passes):
                 nc.tensor.matmul_mx(
@@ -219,6 +221,7 @@ def tile_list_rgg_noneP_kernel(
         message_rows(0, 0, 7)
         message_rows(1, 0, 5)
         gate_rows(1, 0, bank(6))
+        deal_wb_words(1)
         later_accs = message_passes(1, (7, 4, 5, 6))
         weigh_messages(1, later_accs, 0)
         weigh_messages(0, accs, 1)

@@ -65,24 +65,26 @@ def tile_list_rgg_noneP_kernel(
         wc_s = own("wc_s", [P, N], U8)
         wb_s = at(AT_WB_SCALES, "wb_s", [P, N], U8)
         ident = own("ident", [P, P], F32)
+        wgo_rows = own("wgo_rows", [P, P], F32)
         zeros_weights = at(AT_FIRST_LOADS, "zeros_weights", [P, (AT_WA_ROUNDED - AT_FIRST_LOADS) // 4], I32)
         warm_in = keep.tile([P, 1], F32, name="warm_in")
         warm = keep.tile([P, 1], F32, name="warm")
 
         page = [own("page0", [P, T], F32)]
         nc.vector.memset(tab_s[:].bitcast(I32), 0)
+        nc.vector.memset(zeros_weights[:, 0:P], 0)
+        nc.vector.memset(page[0][:, 0 : T // 2], 0.0)
+        nc.vector.tensor_copy(out=wc_s[:].bitcast(I32), in_=zeros_weights[:, 0:P])
+        nc.vector.memset(wgo_rows[:], 0.0)
+        nc.vector.memset(wb_s[:].bitcast(I32), 0)
+        nc.vector.memset(page[0][:, T // 2 : T], 0.0)
         nc.vector.memset(warm_in[:], 0.0)
         nc.scalar.activation(out=warm[:], in_=warm_in[:], func=ACT.Sigmoid)
-        nc.vector.memset(zeros_weights[:, 0:P], 0)
-        nc.vector.memset(page[0][:], 0.0)
-        nc.vector.tensor_copy(out=wc_s[:].bitcast(I32), in_=zeros_weights[:, 0:P])
-        nc.vector.memset(wb_s[:].bitcast(I32), 0)
         make_identity(nc, ident[:])
 
         tab_w = at(AT_FIRST_LOADS + 6 * KB, "tab_w", [P, T], I32)
         wc_w = at(AT_LATER_LOADS, "wc_w", [P, N], I32)
         wb_w = at(AT_FIRST_LOADS, "wb_w", [P, N], I32)
-        wgo_rows = at(AT_FIRST_LOADS + 14 * KB, "wgo_rows", [P, P], F32)
         wa_raw = [
             at(AT_FIRST_LOADS + 2 * KB, "wa_raw0", [P, PACK, N // 2], F32)[:],
             at(AT_LATER_LOADS + 2 * KB, "wa_raw1", [P, 2 * PACK, N // 2], F32)[:, 0:PACK, :],
@@ -94,7 +96,7 @@ def tile_list_rgg_noneP_kernel(
         nc.sync.dma_start(out=wa_raw[0], in_=wa_rows[:, :, 0 : N // 2])
         nc.sync.dma_start(out=tab_w[:], in_=words_of(tab_words))
         load_scale_rows(nc.sync, wc_s, wc_scales[0])
-        nc.sync.dma_start(out=wgo_rows[:], in_=wgo[0 : P * P // J, :].rearrange("o (c p) -> (o c) p", p=P))
+        nc.sync.dma_start(out=wgo_rows[0 : J // P, :], in_=wgo[0:1, :].rearrange("o (c p) -> (o c) p", p=P))
         nc.sync.dma_start(out=wa_raw[1], in_=wa_rows[:, :, N // 2 : N])
         nc.sync.dma_start(out=wc_w[:], in_=words_of(wc_words))
         nc.sync.dma_start(out=wb_w[:], in_=words_of(wb_words))

@@ -27,17 +27,22 @@ CHUNKS = T // CHUNK
 PIECE = CHUNK // 2
 KB = 1024
 
-AT_FIRST_LOADS = 8 * KB
-AT_PAGES = 10 * KB
-AT_LATER_LOADS = 26 * KB
-AT_WA_ROUNDED = 36 * KB
-AT_WB_SCALES = 40 * KB
-AT_TURNED = 43 * KB
+AT_PAGES = 0
+AT_TABLE = 4 * KB
+AT_WB = 16 * KB
+AT_WA_FIRST = 18 * KB
+AT_WC = 22 * KB
+AT_WA_SECOND = 24 * KB
+AT_LOADS_END = 36 * KB
+AT_TURNED = 36 * KB
+AT_WA_ROUNDED = 52 * KB
+AT_WB_SCALES = 56 * KB
+AT_EDGE_WEIGHTS = 60 * KB
 
 
 def load_scale_rows(queue, plane, rows):
-    for q in range(4):
-        queue.dma_start(out=plane[32 * q : 32 * q + 4, :].bitcast(I32), in_=rows[4 * q : 4 * q + 4, :].bitcast(I32))
+    for r in range(4):
+        queue.dma_start(out=plane[r:P:32, :].bitcast(I32), in_=rows[r:16:4, :].bitcast(I32))
 
 
 def words_of(packed):
@@ -65,29 +70,28 @@ def tile_list_rgg_noneP_kernel(
         wc_s = own("wc_s", [P, N], U8)
         wb_s = at(AT_WB_SCALES, "wb_s", [P, N], U8)
         ident = own("ident", [P, P], F32)
-        wgo_rows = own("wgo_rows", [P, P], F32)
-        zeros_weights = at(AT_FIRST_LOADS, "zeros_weights", [P, (AT_WA_ROUNDED - AT_FIRST_LOADS) // 4], I32)
+        wgo_rows = at(AT_EDGE_WEIGHTS, "wgo_rows", [P, P], F32)
+        zeros = at(AT_TABLE, "zeros", [P, (AT_LOADS_END - AT_TABLE) // 4], I32)
         warm_in = keep.tile([P, 1], F32, name="warm_in")
         warm = keep.tile([P, 1], F32, name="warm")
 
         page = [own("page0", [P, T], F32)]
+        nc.vector.memset(zeros[:, 0:P], 0)
         nc.vector.memset(tab_s[:].bitcast(I32), 0)
-        nc.vector.memset(zeros_weights[:, 0:P], 0)
-        nc.vector.memset(page[0][:, 0 : T // 2], 0.0)
-        nc.vector.tensor_copy(out=wc_s[:].bitcast(I32), in_=zeros_weights[:, 0:P])
+        nc.vector.tensor_copy(out=wc_s[:].bitcast(I32), in_=zeros[:, 0:P])
         nc.vector.memset(wgo_rows[:], 0.0)
         nc.vector.memset(wb_s[:].bitcast(I32), 0)
-        nc.vector.memset(page[0][:, T // 2 : T], 0.0)
+        nc.vector.memset(page[0][:], 0.0)
         nc.vector.memset(warm_in[:], 0.0)
         nc.scalar.activation(out=warm[:], in_=warm_in[:], func=ACT.Sigmoid)
         make_identity(nc, ident[:])
 
-        tab_w = at(AT_FIRST_LOADS + 6 * KB, "tab_w", [P, T], I32)
-        wc_w = at(AT_LATER_LOADS, "wc_w", [P, N], I32)
-        wb_w = at(AT_FIRST_LOADS, "wb_w", [P, N], I32)
+        tab_w = at(AT_TABLE, "tab_w", [P, T], I32)
+        wc_w = at(AT_WC, "wc_w", [P, N], I32)
+        wb_w = at(AT_WB, "wb_w", [P, N], I32)
         wa_raw = [
-            at(AT_FIRST_LOADS + 2 * KB, "wa_raw0", [P, PACK, N // 2], F32)[:],
-            at(AT_LATER_LOADS + 2 * KB, "wa_raw1", [P, 2 * PACK, N // 2], F32)[:, 0:PACK, :],
+            at(AT_WA_FIRST, "wa_raw0", [P, PACK, N // 2], F32)[:],
+            at(AT_WA_SECOND, "wa_raw1", [P, 3 * PACK, N // 2], F32)[:, 0:PACK, :],
         ]
         nc.sync.dma_start(out=src_list[:], in_=offs)
         nc.sync.dma_start(out=dst_list[:], in_=offs2)
@@ -97,8 +101,8 @@ def tile_list_rgg_noneP_kernel(
         nc.sync.dma_start(out=tab_w[:], in_=words_of(tab_words))
         load_scale_rows(nc.sync, wc_s, wc_scales[0])
         nc.sync.dma_start(out=wgo_rows[0 : J // P, :], in_=wgo[0:1, :].rearrange("o (c p) -> (o c) p", p=P))
-        nc.sync.dma_start(out=wa_raw[1], in_=wa_rows[:, :, N // 2 : N])
         nc.sync.dma_start(out=wc_w[:], in_=words_of(wc_words))
+        nc.sync.dma_start(out=wa_raw[1], in_=wa_rows[:, :, N // 2 : N])
         nc.sync.dma_start(out=wb_w[:], in_=words_of(wb_words))
         load_scale_rows(nc.sync, wb_s, wb_scales[0])
 
@@ -136,9 +140,8 @@ def tile_list_rgg_noneP_kernel(
         half_cols = [slice(h * LIST_COLS // 2, (h + 1) * LIST_COLS // 2) for h in range(2)]
         tab_u = tab_w[:].bitcast(U32)
         src_scales = own("src_scales", [P, J], U8)
-        dst_scales = own("dst_scales", [P, J], U8)
         src_s = [src_scales[:, h * HALF : (h + 1) * HALF] for h in range(2)]
-        dst_s = [dst_scales[:, h * HALF : (h + 1) * HALF] for h in range(2)]
+        dst_s = [own("dst_s0", [P, HALF], U8)[:]]
         src_w = [own("src_w0", [P, HALF], U32)]
         dst_w = [own("dst_w0", [P, HALF], U32)]
 
@@ -146,18 +149,20 @@ def tile_list_rgg_noneP_kernel(
             nc.vector.tensor_copy(to[h][:], window.indirect(offsets[:, half_cols[h]]))
 
         nc.vector.tensor_copy(src_scales[:], tab_s[:].indirect(src_list[:]))
-        nc.vector.tensor_copy(dst_scales[:], tab_s[:].indirect(dst_list[:]))
+        gather(dst_s, tab_s[:], dst_list, 0)
         gather(src_w, tab_u, src_list, 0)
         gather(dst_w, tab_u, dst_list, 0)
+        dst_s.append(at(AT_EDGE_WEIGHTS, "dst_s1", [P, HALF], U8)[:])
+        gather(dst_s, tab_s[:], dst_list, 1)
         nc.vector.quantize_mx(out=wa_w[:].bitcast(FP8X4), scales=wa_s[:], in_=wa_bf[:])
         nc.vector.tensor_copy(
             out=wbd_s[:].rearrange("p (t m) -> p t m", t=PACK),
             in_=wb_s[:].rearrange("p (m t) -> p t m", t=PACK),
         )
-        dst_w.append(at(AT_WB_SCALES + N // 2 - 2 * KB, "dst_w1", [P, HALF], U32))
-        src_w.append(at(AT_WB_SCALES + N // 2, "src_w1", [P, HALF], U32))
-        gather(dst_w, tab_u, dst_list, 1)
+        src_w.append(at(AT_WB_SCALES + N // 2 - 2 * KB, "src_w1", [P, HALF], U32))
+        dst_w.append(at(AT_WB_SCALES + N // 2, "dst_w1", [P, HALF], U32))
         gather(src_w, tab_u, src_list, 1)
+        gather(dst_w, tab_u, dst_list, 1)
         for t in (1, 2):
             page.append(at(AT_PAGES + 8 * KB * (t - 1), "page%d" % t, [P, T], F32))
             nc.gpsimd.memset(page[t][:], 0.0)
@@ -165,7 +170,7 @@ def tile_list_rgg_noneP_kernel(
 
         msg = [own("msg%d" % t, [P, J], F32) for t in range(PACK)]
         gate = [own("gate%d" % t, [P, J], F32) for t in range(PACK)]
-        turned_at = [AT_LATER_LOADS + 2 * KB * (1 + i) for i in range(BLOCKS)] + [AT_TURNED + 4 * KB * i for i in range(BLOCKS)]
+        turned_at = [AT_WA_SECOND + 4 * KB + 2 * KB * i for i in range(BLOCKS)] + [AT_TURNED + 4 * KB * i for i in range(BLOCKS)]
         turned = {}
 
         def message_passes(h, banks):
@@ -182,19 +187,20 @@ def tile_list_rgg_noneP_kernel(
                 )
             return accs
 
+        def weigh_block(b, acc, g, offset):
+            turned[b, g] = at(offset, "turned%d_%d" % (b, g), [P, 2, P], F32)
+            nc.scalar.activation(
+                out=turned[b, g][:],
+                in_=acc.rearrange("p (m t) -> p t m", t=PACK)[:, 2 * g : 2 * g + 2, :],
+                func=ACT.Copy,
+                scale=wgo_col[:, b : b + 1],
+            )
+
         def weigh_messages(h, accs, g):
             for i, acc in enumerate(accs):
-                b = h * BLOCKS + i
-                turned[b, g] = at(turned_at[b], "turned%d_%d" % (b, g), [P, 2, P], F32)
-                nc.scalar.activation(
-                    out=turned[b, g][:],
-                    in_=acc.rearrange("p (m t) -> p t m", t=PACK)[:, 2 * g : 2 * g + 2, :],
-                    func=ACT.Copy,
-                    scale=wgo_col[:, b : b + 1],
-                )
+                weigh_block(h * BLOCKS + i, acc, g, turned_at[h * BLOCKS + i])
 
-        def message_rows(t, h, index):
-            back = bank(index)
+        def message_rows(t, h, back):
             for i in range(BLOCKS):
                 nc.tensor.transpose(back[:, i * P : (i + 1) * P], turned[h * BLOCKS + i, t // 2][:, t % 2, :], ident[:])
             nc.scalar.copy(out=msg[t][:, h * HALF : (h + 1) * HALF], in_=back)
@@ -219,20 +225,21 @@ def tile_list_rgg_noneP_kernel(
 
         accs = message_passes(0, (0, 1, 2, 3))
         weigh_messages(0, accs, 0)
-        gate_rows(0, 0, bank(4, span=3))
-        message_rows(0, 0, 7)
-        message_rows(1, 0, 5)
+        weigh_block(3, accs[3], 1, turned_at[3] + KB)
+        message_rows(0, 0, bank(7))
+        gate_rows(0, 0, bank(3, span=4))
+        message_rows(1, 0, bank(5))
         gate_rows(1, 0, bank(6))
         deal_wb_words(1)
-        later_accs = message_passes(1, (7, 4, 5, 6))
+        later_accs = message_passes(1, (7, 4, 3, 5))
         weigh_messages(1, later_accs, 0)
-        weigh_messages(0, accs, 1)
-        for t, h, back, za in ((0, 1, 0, 1), (1, 1, 2, 3)):
-            message_rows(t, h, back)
+        weigh_messages(0, accs[0:3], 1)
+        for t, h, back, za in ((0, 1, 0, 6), (1, 1, 1, 2)):
+            message_rows(t, h, bank(back))
             gate_rows(t, h, bank(za))
         weigh_messages(1, later_accs, 1)
-        for t, h, back, za in ((2, 0, 7, 4), (2, 1, 5, 6), (3, 0, 0, 1), (3, 1, 2, 3)):
-            message_rows(t, h, back)
+        for t, h, back, za in ((2, 0, 7, 4), (2, 1, 3, 5), (3, 0, 0, 6), (3, 1, 1, 2)):
+            message_rows(t, h, bank(back))
             gate_rows(t, h, bank(za))
 
         out_rows = out_0.rearrange("(p t) c -> t p c", t=PACK)

@@ -31,7 +31,6 @@ AT_PAGES = 0
 AT_TABLE = 4 * KB
 AT_WB = 16 * KB
 AT_WA_FIRST = 18 * KB
-AT_WC = 22 * KB
 AT_WA_SECOND = 24 * KB
 AT_LOADS_END = 36 * KB
 AT_TURNED = 36 * KB
@@ -71,23 +70,27 @@ def tile_list_rgg_noneP_kernel(
         wb_s = at(AT_WB_SCALES, "wb_s", [P, N], U8)
         ident = own("ident", [P, P], F32)
         wgo_rows = at(AT_EDGE_WEIGHTS, "wgo_rows", [P, P], F32)
-        zeros = at(AT_TABLE, "zeros", [P, (AT_LOADS_END - AT_TABLE) // 4], I32)
+        zeros = [
+            at(AT_TABLE, "zeros_table", [P, P], I32),
+            at(AT_WB, "zeros_weights", [P, (AT_LOADS_END - AT_WB) // 4], I32),
+        ]
         warm_in = keep.tile([P, 1], F32, name="warm_in")
         warm = keep.tile([P, 1], F32, name="warm")
 
         page = [own("page0", [P, T], F32)]
-        nc.vector.memset(zeros[:, 0:P], 0)
+        nc.vector.memset(zeros[0][:], 0)
         nc.vector.memset(tab_s[:].bitcast(I32), 0)
-        nc.vector.tensor_copy(out=wc_s[:].bitcast(I32), in_=zeros[:, 0:P])
         nc.vector.memset(wgo_rows[:], 0.0)
-        nc.vector.memset(wb_s[:].bitcast(I32), 0)
+        nc.vector.tensor_copy(out=wc_s[:].bitcast(I32), in_=zeros[0][:])
+        nc.vector.memset(zeros[1][:, 0:P], 0)
+        nc.vector.tensor_copy(out=wb_s[:].bitcast(I32), in_=zeros[1][:, 0:P])
         nc.vector.memset(page[0][:], 0.0)
         nc.vector.memset(warm_in[:], 0.0)
         nc.scalar.activation(out=warm[:], in_=warm_in[:], func=ACT.Sigmoid)
         make_identity(nc, ident[:])
 
         tab_w = at(AT_TABLE, "tab_w", [P, T], I32)
-        wc_w = at(AT_WC, "wc_w", [P, N], I32)
+        wc_w = own("wc_w", [P, N], I32)
         wb_w = at(AT_WB, "wb_w", [P, N], I32)
         wa_raw = [
             at(AT_WA_FIRST, "wa_raw0", [P, PACK, N // 2], F32)[:],
@@ -95,13 +98,13 @@ def tile_list_rgg_noneP_kernel(
         ]
         nc.sync.dma_start(out=src_list[:], in_=offs)
         nc.sync.dma_start(out=dst_list[:], in_=offs2)
+        nc.sync.dma_start(out=wc_w[:], in_=words_of(wc_words))
         load_scale_rows(nc.sync, tab_s, tab_scales[0])
         wa_rows = wa.rearrange("(p j) n -> p j n", j=PACK)
-        nc.sync.dma_start(out=wa_raw[0], in_=wa_rows[:, :, 0 : N // 2])
         nc.sync.dma_start(out=tab_w[:], in_=words_of(tab_words))
-        load_scale_rows(nc.sync, wc_s, wc_scales[0])
         nc.sync.dma_start(out=wgo_rows[0 : J // P, :], in_=wgo[0:1, :].rearrange("o (c p) -> (o c) p", p=P))
-        nc.sync.dma_start(out=wc_w[:], in_=words_of(wc_words))
+        load_scale_rows(nc.sync, wc_s, wc_scales[0])
+        nc.sync.dma_start(out=wa_raw[0], in_=wa_rows[:, :, 0 : N // 2])
         nc.sync.dma_start(out=wa_raw[1], in_=wa_rows[:, :, N // 2 : N])
         nc.sync.dma_start(out=wb_w[:], in_=words_of(wb_words))
         load_scale_rows(nc.sync, wb_s, wb_scales[0])

@@ -273,8 +273,7 @@ def tile_list_rgg_noneP_kernel(
                 pairs[k][:].bitcast(F32).rearrange("p (u c) -> p c u", u=2)[:, cols, :],
             )
 
-        def quantise_out(piece):
-            k, cols = span(piece, piece)
+        def quantise_out(k, cols):
             nc.vector.quantize_mx(
                 out=codes[k][:, cols].bitcast(FP8X4),
                 scales=out_s[4 * k : P, cols],
@@ -284,8 +283,9 @@ def tile_list_rgg_noneP_kernel(
         def store_codes(k, cols):
             nc.sync.dma_start(out=out_words[:, k * CHUNK : (k + 1) * CHUNK][:, cols], in_=codes[k][:, cols].bitcast(I32))
 
-        merged_late = [span(2, 3), span(4, 4)]
-        placed_early = [span(5, 5), span(6, 7)]
+        merged_late = [span(2, 3), (2, slice(0, P))]
+        placed_early = [(2, slice(P, CHUNK)), span(6, 7)]
+        last_pieces = [(3, slice(PIECE, PIECE + P)), (3, slice(PIECE + P, CHUNK))]
         for h in range(2):
             cols = slice(h * HALF, (h + 1) * HALF)
             for t in range(2):
@@ -310,20 +310,22 @@ def tile_list_rgg_noneP_kernel(
 
         for k, cols in merged_late:
             nc.scalar.copy(out=pair_view(k, 1)[:, cols, 1], in_=page_cols(3, k)[:, cols])
-        for piece in (5, 6, 7):
-            k, cols = span(piece, piece)
+        for k, cols in [(2, slice(P, PIECE)), span(5, 5), span(6, 6)] + last_pieces:
             nc.scalar.copy(out=slot(k, 3)[:, cols], in_=page_cols(3, k)[:, cols])
         for piece in (0, 1):
             nc.vector.tensor_copy(out=slot(0, 3)[:, within(piece)], in_=page_cols(3, 0)[:, within(piece)])
-        quantise_out(0)
-        for piece in range(1, 2 * CHUNKS):
-            if piece + 1 in (2, 3, 4):
-                nc.vector.tensor_copy(*merge_views(*span(piece + 1, piece + 1)))
-            quantise_out(piece)
+        merges = [span(2, 2), span(3, 3), merged_late[1]]
+        quantise_out(*span(0, 0))
+        for piece in range(1, 2 * CHUNKS - 1):
+            if piece <= len(merges):
+                nc.vector.tensor_copy(*merge_views(*merges[piece - 1]))
+            quantise_out(*span(piece, piece))
             if piece in (1, 3, 5):
                 store_codes(*span(piece - 1, piece))
-            if piece in (6, 7):
-                store_codes(*span(piece, piece))
+        quantise_out(*last_pieces[0])
+        store_codes(3, slice(0, PIECE + P))
+        quantise_out(*last_pieces[1])
+        store_codes(*last_pieces[1])
         for q in range(4):
             queue = nc.sync if q % 2 == 0 else nc.scalar
             queue.dma_start(

@@ -29,8 +29,9 @@ KB = 1024
 
 AT_PAGES = 0
 AT_TABLE = 4 * KB
-AT_WB = 16 * KB
-AT_WA_FIRST = 18 * KB
+AT_WC = 16 * KB
+AT_WB = 18 * KB
+AT_WA_FIRST = 20 * KB
 AT_WA_SECOND = 24 * KB
 AT_LOADS_END = 36 * KB
 AT_TURNED = 36 * KB
@@ -71,17 +72,17 @@ def tile_list_rgg_noneP_kernel(
         ident = own("ident", [P, P], F32)
         wgo_rows = at(AT_EDGE_WEIGHTS, "wgo_rows", [P, P], F32)
         zeros = [
-            at(AT_TABLE, "zeros_table", [P, P], I32),
+            at(AT_TABLE, "zeros_table", [P, (AT_WB - AT_TABLE) // 4], I32),
             at(AT_WB, "zeros_weights", [P, (AT_LOADS_END - AT_WB) // 4], I32),
         ]
         warm_in = keep.tile([P, 1], F32, name="warm_in")
         warm = keep.tile([P, 1], F32, name="warm")
 
         page = [own("page0", [P, T], F32)]
-        nc.vector.memset(zeros[0][:], 0)
         nc.vector.memset(tab_s[:].bitcast(I32), 0)
+        nc.vector.memset(zeros[0][:, 0:P], 0)
         nc.vector.memset(wgo_rows[:], 0.0)
-        nc.vector.tensor_copy(out=wc_s[:].bitcast(I32), in_=zeros[0][:])
+        nc.vector.tensor_copy(out=wc_s[:].bitcast(I32), in_=zeros[0][:, 0:P])
         nc.vector.memset(zeros[1][:, 0:P], 0)
         nc.vector.tensor_copy(out=wb_s[:].bitcast(I32), in_=zeros[1][:, 0:P])
         nc.vector.memset(page[0][:], 0.0)
@@ -90,7 +91,7 @@ def tile_list_rgg_noneP_kernel(
         make_identity(nc, ident[:])
 
         tab_w = at(AT_TABLE, "tab_w", [P, T], I32)
-        wc_w = own("wc_w", [P, N], I32)
+        wc_w = at(AT_WC, "wc_w", [P, N], I32)
         wb_w = at(AT_WB, "wb_w", [P, N], I32)
         wa_raw = [
             at(AT_WA_FIRST, "wa_raw0", [P, PACK, N // 2], F32)[:],
@@ -98,8 +99,8 @@ def tile_list_rgg_noneP_kernel(
         ]
         nc.sync.dma_start(out=src_list[:], in_=offs)
         nc.sync.dma_start(out=dst_list[:], in_=offs2)
-        nc.sync.dma_start(out=wc_w[:], in_=words_of(wc_words))
         load_scale_rows(nc.sync, tab_s, tab_scales[0])
+        nc.sync.dma_start(out=wc_w[:], in_=words_of(wc_words))
         wa_rows = wa.rearrange("(p j) n -> p j n", j=PACK)
         nc.sync.dma_start(out=tab_w[:], in_=words_of(tab_words))
         nc.sync.dma_start(out=wgo_rows[0 : J // P, :], in_=wgo[0:1, :].rearrange("o (c p) -> (o c) p", p=P))
@@ -126,8 +127,8 @@ def tile_list_rgg_noneP_kernel(
         wa_s = own("wa_s", [P, N], U8)
         for c in range(2):
             nc.scalar.copy(
-                out=wa_bf[:].rearrange("p (t m j) -> p m t j", t=PACK, j=PACK)[:, c * P // 2 : (c + 1) * P // 2, :, :],
-                in_=wa_raw[c].rearrange("p j (m t) -> p m t j", t=PACK),
+                out=wa_bf[:].rearrange("p (t m j) -> p m j t", t=PACK, j=PACK)[:, c * P // 2 : (c + 1) * P // 2, :, :],
+                in_=wa_raw[c].rearrange("p j (m t) -> p m j t", t=PACK),
             )
 
         wbd_w = [own("wbd_w%d" % g, [P, 2 * P], U32) for g in range(2)]

@@ -38,6 +38,7 @@ AT_TURNED = 36 * KB
 AT_WA_ROUNDED = 52 * KB
 AT_WB_SCALES = 56 * KB
 AT_EDGE_WEIGHTS = 60 * KB
+AT_FIRST_GATE = 62 * KB
 
 
 def load_scale_rows(queue, plane, rows):
@@ -117,9 +118,11 @@ def tile_list_rgg_noneP_kernel(
             made.append(acc)
             return acc[:, 0, :]
 
-        wgo_bank = bank(7)
+        wgo_bank = bank(4)
         nc.tensor.transpose(wgo_bank[:, 0:P], wgo_rows[:], ident[:])
         wgo_col = keep.tile([P, J // P], F32, name="wgo_col")
+        wgo_first = at(AT_FIRST_GATE, "wgo_first", [P, BLOCKS], F32)
+        nc.scalar.copy(out=wgo_first[:], in_=wgo_bank[:, 0:BLOCKS])
         nc.scalar.copy(out=wgo_col[:], in_=wgo_bank[:, 0 : J // P])
 
         wa_bf = at(AT_WA_ROUNDED, "wa_bf", [P, N * PACK], BF16)
@@ -131,7 +134,7 @@ def tile_list_rgg_noneP_kernel(
                 in_=wa_raw[c].rearrange("p j (m t) -> p m j t", t=PACK),
             )
 
-        wbd_w = [own("wbd_w%d" % g, [P, 2 * P], U32) for g in range(2)]
+        wbd_w = [own("wbd_w0", [P, 2 * P], U32)]
         wbd_s = own("wbd_s", [P, N], U8)
 
         def deal_wb_words(g):
@@ -174,6 +177,7 @@ def tile_list_rgg_noneP_kernel(
 
         msg = [own("msg%d" % t, [P, J], F32) for t in range(PACK)]
         gate = [own("gate%d" % t, [P, J], F32) for t in range(PACK)]
+        gates = {(t, h): gate[t][:, h * HALF : (h + 1) * HALF] for t in range(PACK) for h in range(2)}
         turned_at = [AT_WA_SECOND + 4 * KB + 2 * KB * i for i in range(BLOCKS)] + [AT_TURNED + 4 * KB * i for i in range(BLOCKS)]
         turned = {}
 
@@ -191,18 +195,19 @@ def tile_list_rgg_noneP_kernel(
                 )
             return accs
 
-        def weigh_block(b, acc, g, offset):
-            turned[b, g] = at(offset, "turned%d_%d" % (b, g), [P, 2, P], F32)
+        def weigh_block(b, acc, g, offset, weights):
+            depth = PACK if (b, g) == (0, 0) else 2
+            turned[b, g] = at(offset, "turned%d_%d" % (b, g), [P, depth, P], F32)
             nc.scalar.activation(
-                out=turned[b, g][:],
+                out=turned[b, g][:, 0:2, :],
                 in_=acc.rearrange("p (m t) -> p t m", t=PACK)[:, 2 * g : 2 * g + 2, :],
                 func=ACT.Copy,
-                scale=wgo_col[:, b : b + 1],
+                scale=weights[:, b : b + 1],
             )
 
-        def weigh_messages(h, accs, g):
+        def weigh_messages(h, accs, g, weights):
             for i, acc in enumerate(accs):
-                weigh_block(h * BLOCKS + i, acc, g, turned_at[h * BLOCKS + i])
+                weigh_block(h * BLOCKS + i, acc, g, turned_at[h * BLOCKS + i], weights)
 
         def message_rows(t, h, back):
             for i in range(BLOCKS):
@@ -225,23 +230,25 @@ def tile_list_rgg_noneP_kernel(
                     start=n == 0,
                     stop=n == 1,
                 )
-            nc.scalar.activation(out=gate[t][:, h * HALF : (h + 1) * HALF], in_=za, func=ACT.Sigmoid)
+            nc.scalar.activation(out=gates[t, h], in_=za, func=ACT.Sigmoid)
 
         accs = message_passes(0, (0, 1, 2, 3))
-        weigh_messages(0, accs, 0)
-        weigh_block(3, accs[3], 1, turned_at[3] + KB)
+        weigh_messages(0, accs, 0, wgo_first)
+        gates[0, 0] = at(AT_FIRST_GATE, "first_gate", [P, HALF], F32)[:]
         message_rows(0, 0, bank(7))
-        gate_rows(0, 0, bank(3, span=4))
+        gate_rows(0, 0, bank(4, span=3))
+        weigh_block(3, accs[3], 1, turned_at[3] + KB, wgo_col)
         message_rows(1, 0, bank(5))
         gate_rows(1, 0, bank(6))
-        deal_wb_words(1)
         later_accs = message_passes(1, (7, 4, 3, 5))
-        weigh_messages(1, later_accs, 0)
-        weigh_messages(0, accs[0:3], 1)
+        weigh_messages(1, later_accs, 0, wgo_col)
+        weigh_messages(0, accs[0:3], 1, wgo_col)
         for t, h, back, za in ((0, 1, 0, 6), (1, 1, 1, 2)):
             message_rows(t, h, bank(back))
             gate_rows(t, h, bank(za))
-        weigh_messages(1, later_accs, 1)
+        wbd_w.append(at(turned_at[0] + KB, "wbd_w1", [P, 2 * P], U32))
+        deal_wb_words(1)
+        weigh_messages(1, later_accs, 1, wgo_col)
         for t, h, back, za in ((2, 0, 7, 4), (2, 1, 3, 5), (3, 0, 0, 6), (3, 1, 1, 2)):
             message_rows(t, h, bank(back))
             gate_rows(t, h, bank(za))
@@ -287,10 +294,11 @@ def tile_list_rgg_noneP_kernel(
         merged_late = [span(2, 3), (2, slice(0, P))]
         placed_early = [(2, slice(P, CHUNK)), span(6, 7)]
         last_pieces = [(3, slice(PIECE, PIECE + P)), (3, slice(PIECE + P, CHUNK))]
+        nc.gpsimd.memset(pair_view(0, 1), 0.0)
         for h in range(2):
             cols = slice(h * HALF, (h + 1) * HALF)
             for t in range(2):
-                nc.vector.tensor_tensor(page[t][:].indirect(dst_list[:, half_cols[h]]), gate[t][:, cols], msg[t][:, cols], MULT)
+                nc.vector.tensor_tensor(page[t][:].indirect(dst_list[:, half_cols[h]]), gates[t, h], msg[t][:, cols], MULT)
         for t in range(2):
             nc.sync.dma_start(out=out_rows[t], in_=page[t][:])
             for k in range(CHUNKS):
@@ -300,7 +308,7 @@ def tile_list_rgg_noneP_kernel(
             nc.scalar.copy(out=to[:, :, 0], in_=source[:, :, 0])
         nc.vector.tensor_tensor(page[2][:].indirect(dst_list[:]), gate[2][:], msg[2][:], MULT)
         nc.sync.dma_start(out=out_rows[2], in_=page[2][:])
-        nc.scalar.copy(out=pair_view(0, 1), in_=page_cols(2, 0).unsqueeze(2).to_broadcast([P, CHUNK, 2]))
+        nc.scalar.copy(out=pair_view(0, 1)[:, :, 0], in_=page_cols(2, 0))
         nc.scalar.copy(*merge_views(0, slice(0, CHUNK)))
         for k, cols in merged_late:
             nc.scalar.copy(out=pair_view(k, 1)[:, cols, 0], in_=page_cols(2, k)[:, cols])

@@ -73,8 +73,8 @@ def tile_list_rgg_noneP_kernel(
         ident = own("ident", [P, P], F32)
         wgo_rows = at(AT_EDGE_WEIGHTS, "wgo_rows", [P, P], F32)
         zeros = [
-            at(AT_TABLE, "zeros_table", [P, (AT_WB - AT_TABLE) // 4], I32),
-            at(AT_WB, "zeros_weights", [P, (AT_LOADS_END - AT_WB) // 4], I32),
+            at(AT_TABLE, "zeros_table", [P, P], I32),
+            at(AT_WC, "zeros_weights", [P, (AT_LOADS_END - AT_WC) // 4], I32),
         ]
         warm_in = keep.tile([P, 1], F32, name="warm_in")
         warm = keep.tile([P, 1], F32, name="warm")
@@ -101,13 +101,13 @@ def tile_list_rgg_noneP_kernel(
         nc.sync.dma_start(out=src_list[:], in_=offs)
         nc.sync.dma_start(out=dst_list[:], in_=offs2)
         load_scale_rows(nc.sync, tab_s, tab_scales[0])
-        nc.sync.dma_start(out=wc_w[:], in_=words_of(wc_words))
         wa_rows = wa.rearrange("(p j) n -> p j n", j=PACK)
         nc.sync.dma_start(out=tab_w[:], in_=words_of(tab_words))
         nc.sync.dma_start(out=wgo_rows[0 : J // P, :], in_=wgo[0:1, :].rearrange("o (c p) -> (o c) p", p=P))
         load_scale_rows(nc.sync, wc_s, wc_scales[0])
         nc.sync.dma_start(out=wa_raw[0], in_=wa_rows[:, :, 0 : N // 2])
         nc.sync.dma_start(out=wa_raw[1], in_=wa_rows[:, :, N // 2 : N])
+        nc.sync.dma_start(out=wc_w[:], in_=words_of(wc_words))
         nc.sync.dma_start(out=wb_w[:], in_=words_of(wb_words))
         load_scale_rows(nc.sync, wb_s, wb_scales[0])
 

from contextlib import ExitStack

import concourse.mybir as mybir
from concourse.masks import make_identity

K, N, T, J = 512, 512, 2048, 1024
FLOPS = 3 * 2 * K * N * J

F32 = mybir.dt.float32
BF16 = mybir.dt.bfloat16
I32 = mybir.dt.int32
U32 = mybir.dt.uint32
U16 = mybir.dt.uint16
U8 = mybir.dt.uint8
FP8X4 = mybir.dt.float8_e4m3fn_x4
ACT = mybir.ActivationFunctionType
MULT = mybir.AluOpType.mult

P = 128
PACK = 4
HALF = J // 2
BLOCKS = HALF // P
LIST_COLS = J // 16
BANK = 2048
CHUNK = 512
CHUNKS = T // CHUNK
PIECE = CHUNK // 2
KB = 1024

AT_PAGES = 0
AT_TABLE = 4 * KB
AT_WC = 16 * KB
AT_WB = 18 * KB
AT_WA_FIRST = 20 * KB
AT_WA_SECOND = 24 * KB
AT_LOADS_END = 36 * KB
AT_TURNED = 36 * KB
AT_WA_ROUNDED = 52 * KB
AT_WB_SCALES = 56 * KB
AT_EDGE_WEIGHTS = 60 * KB
AT_FIRST_GATE = 62 * KB


def load_scale_rows(queue, plane, rows):
    for r in range(4):
        queue.dma_start(out=plane[r:P:32, :].bitcast(I32), in_=rows[r:16:4, :].bitcast(I32))


def words_of(packed):
    return packed[0].rearrange("p c i -> p (c i)").bitcast(I32)


def tile_list_rgg_noneP_kernel(
    tc, tab_words, tab_scales, wa, wb_words, wb_scales, wc_words, wc_scales, wgo, offs, offs2, out_0, out_1, out_2
):
    nc = tc.nc
    with ExitStack() as ctx:
        keep = ctx.enter_context(tc.tile_pool(name="keep", bufs=1))
        placed = ctx.enter_context(tc.tile_pool(name="placed", bufs=1))
        psum = ctx.enter_context(tc.psum_pool(name="psum", bufs=1))

        def own(name, shape, dtype):
            return keep.tile(shape, dtype, name=name, align_bytes=64)

        def at(offset, name, shape, dtype):
            return placed.tile(shape, dtype, name=name, offset=offset, align_bytes=64)

        src_list = keep.tile([P, LIST_COLS], U16, name="src_list")
        dst_list = keep.tile([P, LIST_COLS], U16, name="dst_list")
        tab_s = own("tab_s", [P, T], U8)
        wc_s = own("wc_s", [P, N], U8)
        wb_s = at(AT_WB_SCALES, "wb_s", [P, N], U8)
        ident = own("ident", [P, P], F32)
        wgo_rows = at(AT_EDGE_WEIGHTS, "wgo_rows", [P, P], F32)
        zeros = [
            at(AT_TABLE, "zeros_table", [P, P], I32),
            at(AT_WC, "zeros_weights", [P, (AT_LOADS_END - AT_WC) // 4], I32),
        ]
        warm_in = keep.tile([P, 1], F32, name="warm_in")
        warm = keep.tile([P, 1], F32, name="warm")

        page = [own("page0", [P, T], F32)]
        nc.vector.memset(tab_s[:].bitcast(I32), 0)
        nc.vector.memset(zeros[0][:, 0:P], 0)
        nc.vector.memset(wgo_rows[:], 0.0)
        nc.vector.tensor_copy(out=wc_s[:].bitcast(I32), in_=zeros[0][:, 0:P])
        nc.vector.memset(zeros[1][:, 0:P], 0)
        nc.vector.tensor_copy(out=wb_s[:].bitcast(I32), in_=zeros[1][:, 0:P])
        nc.vector.memset(page[0][:], 0.0)
        nc.vector.memset(warm_in[:], 0.0)
        nc.scalar.activation(out=warm[:], in_=warm_in[:], func=ACT.Sigmoid)
        make_identity(nc, ident[:])

        tab_w = at(AT_TABLE, "tab_w", [P, T], I32)
        wc_w = at(AT_WC, "wc_w", [P, N], I32)
        wb_w = at(AT_WB, "wb_w", [P, N], I32)
        wa_raw = [
            at(AT_WA_FIRST, "wa_raw0", [P, PACK, N // 2], F32)[:],
            at(AT_WA_SECOND, "wa_raw1", [P, 3 * PACK, N // 2], F32)[:, 0:PACK, :],
        ]
        nc.sync.dma_start(out=src_list[:], in_=offs)
        nc.sync.dma_start(out=dst_list[:], in_=offs2)
        load_scale_rows(nc.sync, tab_s, tab_scales[0])
        wa_rows = wa.rearrange("(p j) n -> p j n", j=PACK)
        nc.sync.dma_start(out=tab_w[:], in_=words_of(tab_words))
        nc.sync.dma_start(out=wgo_rows[0 : J // P, :], in_=wgo[0:1, :].rearrange("o (c p) -> (o c) p", p=P))
        load_scale_rows(nc.sync, wc_s, wc_scales[0])
        nc.sync.dma_start(out=wa_raw[0], in_=wa_rows[:, :, 0 : N // 2])
        nc.sync.dma_start(out=wa_raw[1], in_=wa_rows[:, :, N // 2 : N])
        nc.sync.dma_start(out=wc_w[:], in_=words_of(wc_words))
        nc.sync.dma_start(out=wb_w[:], in_=words_of(wb_words))
        load_scale_rows(nc.sync, wb_s, wb_scales[0])

        made = []

        def bank(index, span=1):
            acc = psum.tile([P, span, HALF], F32, name="acc%d" % len(made), offset=index * BANK)
            made.append(acc)
            return acc[:, 0, :]

        wgo_bank = bank(4)
        nc.tensor.transpose(wgo_bank[:, 0:P], wgo_rows[:], ident[:])
        wgo_col = keep.tile([P, J // P], F32, name="wgo_col")
        wgo_first = at(AT_FIRST_GATE, "wgo_first", [P, BLOCKS], F32)
        nc.scalar.copy(out=wgo_first[:], in_=wgo_bank[:, 0:BLOCKS])
        nc.scalar.copy(out=wgo_col[:], in_=wgo_bank[:, 0 : J // P])

        wa_bf = at(AT_WA_ROUNDED, "wa_bf", [P, N * PACK], BF16)
        wa_w = own("wa_w", [P, N], U32)
        wa_s = own("wa_s", [P, N], U8)
        for c in range(2):
            nc.scalar.copy(
                out=wa_bf[:].rearrange("p (t m j) -> p m j t", t=PACK, j=PACK)[:, c * P // 2 : (c + 1) * P // 2, :, :],
                in_=wa_raw[c].rearrange("p j (m t) -> p m j t", t=PACK),
            )

        wbd_w = [own("wbd_w0", [P, 2 * P], U32)]
        wbd_s = own("wbd_s", [P, N], U8)

        def deal_wb_words(g):
            nc.scalar.copy(
                out=wbd_w[g][:].rearrange("p (t m) -> p m t", t=2),
                in_=wb_w[:].bitcast(U32).rearrange("p (m t) -> p m t", t=PACK)[:, :, 2 * g : 2 * g + 2],
            )

        deal_wb_words(0)
        half_cols = [slice(h * LIST_COLS // 2, (h + 1) * LIST_COLS // 2) for h in range(2)]
        tab_u = tab_w[:].bitcast(U32)
        src_scales = own("src_scales", [P, J], U8)
        src_s = [src_scales[:, h * HALF : (h + 1) * HALF] for h in range(2)]
        dst_s = [own("dst_s0", [P, HALF], U8)[:]]
        src_w = [own("src_w0", [P, HALF], U32)]
        dst_w = [own("dst_w0", [P, HALF], U32)]

        def gather(to, window, offsets, h):
            nc.vector.tensor_copy(to[h][:], window.indirect(offsets[:, half_cols[h]]))

        nc.vector.tensor_copy(src_scales[:], tab_s[:].indirect(src_list[:]))
        gather(dst_s, tab_s[:], dst_list, 0)
        gather(src_w, tab_u, src_list, 0)
        gather(dst_w, tab_u, dst_list, 0)
        dst_s.append(at(AT_EDGE_WEIGHTS, "dst_s1", [P, HALF], U8)[:])
        gather(dst_s, tab_s[:], dst_list, 1)
        nc.vector.quantize_mx(out=wa_w[:].bitcast(FP8X4), scales=wa_s[:], in_=wa_bf[:])
        nc.vector.tensor_copy(
            out=wbd_s[:].rearrange("p (t m) -> p t m", t=PACK),
            in_=wb_s[:].rearrange("p (m t) -> p t m", t=PACK),
        )
        src_w.append(at(AT_WB_SCALES + N // 2 - 2 * KB, "src_w1", [P, HALF], U32))
        dst_w.append(at(AT_WB_SCALES + N // 2, "dst_w1", [P, HALF], U32))
        gather(src_w, tab_u, src_list, 1)
        gather(dst_w, tab_u, dst_list, 1)
        for t in (1, 2):
            page.append(at(AT_PAGES + 8 * KB * (t - 1), "page%d" % t, [P, T], F32))
            nc.gpsimd.memset(page[t][:], 0.0)
        page.append(page[0])

        msg = [own("msg%d" % t, [P, J], F32) for t in range(PACK)]
        gate = [own("gate%d" % t, [P, J], F32) for t in range(PACK)]
        gates = {(t, h): gate[t][:, h * HALF : (h + 1) * HALF] for t in range(PACK) for h in range(2)}
        turned_at = [AT_WA_SECOND + 4 * KB + 2 * KB * i for i in range(BLOCKS)] + [AT_TURNED + 4 * KB * i for i in range(BLOCKS)]
        turned = {}

        def message_passes(h, banks):
            accs = [bank(i) for i in banks]
            for i, acc in enumerate(accs):
                nc.tensor.matmul_mx(
                    out=acc,
                    lhsT=src_w[h][:, i * P : (i + 1) * P].bitcast(FP8X4),
                    lhsT_scale=src_s[h][:, i * P : (i + 1) * P],
                    rhs=wc_w[:].bitcast(FP8X4),
                    rhs_scale=wc_s[:],
                    start=True,
                    stop=True,
                )
            return accs

        def weigh_block(b, acc, g, offset, weights):
            depth = PACK if (b, g) == (0, 0) else 2
            turned[b, g] = at(offset, "turned%d_%d" % (b, g), [P, depth, P], F32)
            nc.scalar.activation(
                out=turned[b, g][:, 0:2, :],
                in_=acc.rearrange("p (m t) -> p t m", t=PACK)[:, 2 * g : 2 * g + 2, :],
                func=ACT.Copy,
                scale=weights[:, b : b + 1],
            )

        def weigh_messages(h, accs, g, weights):
            for i, acc in enumerate(accs):
                weigh_block(h * BLOCKS + i, acc, g, turned_at[h * BLOCKS + i], weights)

        def message_rows(t, h, back):
            for i in range(BLOCKS):
                nc.tensor.transpose(back[:, i * P : (i + 1) * P], turned[h * BLOCKS + i, t // 2][:, t % 2, :], ident[:])
            nc.scalar.copy(out=msg[t][:, h * HALF : (h + 1) * HALF], in_=back)

        def gate_rows(t, h, za):
            rows = slice(t * P, (t + 1) * P)
            passes = [
                (wa_w[:, rows], wa_s[:, rows], dst_w[h], dst_s[h]),
                (wbd_w[t // 2][:, t % 2 * P : (t % 2 + 1) * P], wbd_s[:, rows], src_w[h], src_s[h]),
            ]
            for n, (w_words, w_scales, v_words, v_scales) in enumerate(passes):
                nc.tensor.matmul_mx(
                    out=za,
                    lhsT=w_words.bitcast(FP8X4),
                    lhsT_scale=w_scales,
                    rhs=v_words[:].bitcast(FP8X4),
                    rhs_scale=v_scales,
                    start=n == 0,
                    stop=n == 1,
                )
            nc.scalar.activation(out=gates[t, h], in_=za, func=ACT.Sigmoid)

        accs = message_passes(0, (0, 1, 2, 3))
        weigh_messages(0, accs, 0, wgo_first)
        gates[0, 0] = at(AT_FIRST_GATE, "first_gate", [P, HALF], F32)[:]
        message_rows(0, 0, bank(7))
        gate_rows(0, 0, bank(4, span=3))
        weigh_block(3, accs[3], 1, turned_at[3] + KB, wgo_col)
        message_rows(1, 0, bank(5))
        gate_rows(1, 0, bank(6))
        later_accs = message_passes(1, (7, 4, 3, 5))
        weigh_messages(1, later_accs, 0, wgo_col)
        weigh_messages(0, accs[0:3], 1, wgo_col)
        for t, h, back, za in ((0, 1, 0, 6), (1, 1, 1, 2)):
            message_rows(t, h, bank(back))
            gate_rows(t, h, bank(za))
        wbd_w.append(at(turned_at[0] + KB, "wbd_w1", [P, 2 * P], U32))
        deal_wb_words(1)
        weigh_messages(1, later_accs, 1, wgo_col)
        for t, h, back, za in ((2, 0, 7, 4), (2, 1, 3, 5), (3, 0, 0, 6), (3, 1, 1, 2)):
            message_rows(t, h, bank(back))
            gate_rows(t, h, bank(za))

        out_rows = out_0.rearrange("(p t) c -> t p c", t=PACK)
        out_words = words_of(out_1)
        pairs = [at(AT_TURNED + 4 * KB * k, "pairs%d" % k, [P, 2 * CHUNK * 2], BF16) for k in range(CHUNKS)]
        rounded = [own("rounded%d" % k, [P, CHUNK * PACK], BF16) for k in range(CHUNKS)]
        codes = [own("codes%d" % k, [P, CHUNK], U32) for k in range(CHUNKS)]
        out_s = own("out_s", [P, CHUNK], U8)

        def within(piece):
            return slice(piece % 2 * PIECE, (piece % 2 + 1) * PIECE)

        def span(first, last):
            return first // 2, slice(within(first).start, within(last).stop)

        def pair_view(k, u):
            return pairs[k][:].rearrange("p (u c e) -> p u c e", u=2, e=2)[:, u, :, :]

        def page_cols(t, k):
            return page[t][:, k * CHUNK : (k + 1) * CHUNK]

        def slot(k, t):
            return rounded[k][:].rearrange("p (c t) -> p c t", t=PACK)[:, :, t]

        def merge_views(k, cols):
            return (
                rounded[k][:].bitcast(F32).rearrange("p (c u) -> p c u", u=2)[:, cols, :],
                pairs[k][:].bitcast(F32).rearrange("p (u c) -> p c u", u=2)[:, cols, :],
            )

        def quantise_out(k, cols):
            nc.vector.quantize_mx(
                out=codes[k][:, cols].bitcast(FP8X4),
                scales=out_s[4 * k : P, cols],
                in_=rounded[k][:, PACK * cols.start : PACK * cols.stop],
            )

        def store_codes(k, cols):
            nc.sync.dma_start(out=out_words[:, k * CHUNK : (k + 1) * CHUNK][:, cols], in_=codes[k][:, cols].bitcast(I32))

        merged_late = [span(2, 3), (2, slice(0, P))]
        placed_early = [(2, slice(P, CHUNK)), span(6, 7)]
        last_pieces = [(3, slice(PIECE, PIECE + P)), (3, slice(PIECE + P, CHUNK))]
        nc.gpsimd.memset(pair_view(0, 1), 0.0)
        for h in range(2):
            cols = slice(h * HALF, (h + 1) * HALF)
            for t in range(2):
                nc.vector.tensor_tensor(page[t][:].indirect(dst_list[:, half_cols[h]]), gates[t, h], msg[t][:, cols], MULT)
        for t in range(2):
            nc.sync.dma_start(out=out_rows[t], in_=page[t][:])
            for k in range(CHUNKS):
                nc.scalar.copy(out=pair_view(k, 0)[:, :, t], in_=page_cols(t, k))
        for k, cols in placed_early:
            to, source = merge_views(k, cols)
            nc.scalar.copy(out=to[:, :, 0], in_=source[:, :, 0])
        nc.vector.tensor_tensor(page[2][:].indirect(dst_list[:]), gate[2][:], msg[2][:], MULT)
        nc.sync.dma_start(out=out_rows[2], in_=page[2][:])
        nc.scalar.copy(out=pair_view(0, 1)[:, :, 0], in_=page_cols(2, 0))
        nc.scalar.copy(*merge_views(0, slice(0, CHUNK)))
        for k, cols in merged_late:
            nc.scalar.copy(out=pair_view(k, 1)[:, cols, 0], in_=page_cols(2, k)[:, cols])
        for k, cols in placed_early:
            nc.scalar.copy(out=slot(k, 2)[:, cols], in_=page_cols(2, k)[:, cols])
        nc.vector.tensor_tensor(page[3][:].indirect(dst_list[:]), gate[3][:], msg[3][:], MULT)
        nc.sync.dma_start(out=out_rows[3], in_=page[3][:])

        for k, cols in merged_late:
            nc.scalar.copy(out=pair_view(k, 1)[:, cols, 1], in_=page_cols(3, k)[:, cols])
        for k, cols in [(2, slice(P, PIECE)), span(5, 5), span(6, 6)] + last_pieces:
            nc.scalar.copy(out=slot(k, 3)[:, cols], in_=page_cols(3, k)[:, cols])
        for piece in (0, 1):
            nc.vector.tensor_copy(out=slot(0, 3)[:, within(piece)], in_=page_cols(3, 0)[:, within(piece)])
        merges = [span(2, 2), span(3, 3), merged_late[1]]
        quantise_out(*span(0, 0))
        for piece in range(1, 2 * CHUNKS - 1):
            if piece <= len(merges):
                nc.vector.tensor_copy(*merge_views(*merges[piece - 1]))
            quantise_out(*span(piece, piece))
            if piece in (1, 3, 5):
                store_codes(*span(piece - 1, piece))
        quantise_out(*last_pieces[0])
        store_codes(3, slice(0, PIECE + P))
        quantise_out(*last_pieces[1])
        store_codes(*last_pieces[1])
        for q in range(4):
            queue = nc.sync if q % 2 == 0 else nc.scalar
            queue.dma_start(
                out=out_2[0][4 * q : 4 * q + 4, :].bitcast(I32).rearrange("r (k c) -> k r c", k=CHUNKS),
                in_=out_s[32 * q : 32 * q + 4 * CHUNKS, :].bitcast(I32),
            )
